import numpy as np, ml_dtypes
CORES = [3,7,11,15,131,135,139,143]
N = 8
BF = ml_dtypes.bfloat16
V, S, Q, RO, W = 1024, 4, 256, 4, 1792
def pack(res, cap, B, T, K, wt, ka):
    w = B + 4096 * T - 65536 * K
    return {"res": np.ascontiguousarray(res).reshape(N, 128, W).astype(np.float32).astype(BF), "cap": np.ascontiguousarray(cap).reshape(N, 128, V).astype(np.float32).astype(BF),
            "br": np.ascontiguousarray(w).reshape(N, 128, V).astype(np.int32), "wt": np.ascontiguousarray(wt).reshape(N, 128, 1).astype(np.int32), "ka": np.ascontiguousarray(ka).reshape(N, 128, 1).astype(np.int32)}
def parts(rng):
    sh = (N, 8, 16, V)
    res = (rng.integers(4, 29, (N, 8, 1, W)) * rng.random((N, 8, 16, W))).astype(np.int64)
    heavy = (rng.random((N, 8, 1, W)) < 0.06) & (rng.random((N, 8, 16, W)) < 0.7)
    res = np.where(heavy, rng.integers(0, 256, res.shape), res)
    cap = rng.integers(0, 64, sh); dead = rng.choice(np.array([0.0, 0.25, 0.5]), (N, 8, 1, 1))
    B = rng.integers(0, W, sh); T = np.where(rng.random(sh) < dead, 0, rng.integers(0, 16, sh)); K = np.where(rng.random(sh) < 0.5, 0, rng.integers(0, 16, sh))
    return res, cap, B, T, K, rng.integers(0, 256, (N, 8, 16, 1)), rng.integers(0, V, (N, 8, 16, 1))
def setup_inputs(rng):
    return pack(*parts(rng))
def setup_inputs_corners(rng):
    res, cap, B, T, K, wt, ka = parts(rng)
    v = np.arange(V); t0 = v % S + 1; row = np.arange(16).reshape(16, 1)
    res[..., W - 16:] = np.where(row < np.arange(16), 200, 0)
    res[:, 5, :, 0:V:2] = 255; res[:, 6, :, 0:V:2] = 0; cap[:, 6, :, ::2] = 63
    cl = rng.integers(0, 9, (N, 8, 1, V)); one = rng.integers(0, 16, (N, 8, 1, V)); near = W - 16 + rng.integers(3, 7, (N, 8, 1, V)); same = rng.integers(0, W, (N, 8, 1, V))
    T = np.where(cl == 0, t0 - 1, T); K = np.where(cl == 0, 0, K)
    T = np.where(cl == 1, 15, T); K = np.where(cl == 1, 0, K)
    T = np.where(cl == 2, np.where(row % 2 == 0, t0, t0 - 1), T); K = np.where(cl == 2, 0, K)
    T = np.where(cl == 3, 15, T); K = np.where(cl == 3, np.where(row % 2 == 0, t0 - 1, t0), K)
    T = np.where(cl == 4, np.where(row == one, 15, 0), T); K = np.where(cl == 4, 0, K); B = np.where(cl == 4, near, B); cap = np.where(cl == 4, 63, cap)
    T = np.where(cl == 5, 15, T); K = np.where(cl == 5, 0, K); B = np.where(cl == 5, same, B)
    cap = np.where(cl == 5, np.minimum(np.take_along_axis(res, same, 3), 63), cap)
    chain = np.where(row == 0, v, np.where(row == 1, np.maximum(v - 1, 0), np.where(row == 2, W - 1, np.where(row == 3, 0, V))))
    T = np.where(cl == 6, np.where(row < 5, 15, 0), T); K = np.where(cl == 6, 0, K); B = np.where(cl == 6, chain, B)
    two = (cl == 7) & ((row == 3) | (row == 15))
    T = np.where(two, 15, T); K = np.where(two, 0, K); B = np.where(two, near, B); cap = np.where(cl == 7, 63, cap)
    q = rng.permutation(N); T[q[0], 7] = 0; T[q[1], 7] = 15; K[q[1], 7] = 0
    wt[:, 0] = 0; wt[:, 1] = 255; ka[:, 2] = 0; ka[:, 3] = V - 1; ka[:, 4] = rng.choice(np.array([0, V >> 1]), (N, 16, 1))
    return pack(res, cap, B, T, K, wt, ka)
def setup_inputs_ends(rng):
    sh = (N, 8, 16, V); lane = np.arange(16).reshape(16, 1)
    kd = rng.choice(6, (N, 8, 1, W), p=[0.38, 0.12, 0.25, 0.1, 0.08, 0.07])
    kd[:, :, 0, W - 1] = np.where(np.arange(8) % 2 == 1, 1, 2); kd[:, 7, 0, V - 1] = 5; kd[:, 7, 0, V - 2] = 4
    rot = (lane + rng.integers(0, 16, (N, 8, 1, W))) % 16; some = 255 * (rng.random((N, 8, 16, W)) < 0.2)
    res = np.where(kd == 1, 255, np.where(kd == 2, some, np.where(kd == 3, 63, np.where(kd == 4, np.where(rot < 4, 255, 63), np.where(kd == 5, np.where(rot < 5, 255, 63), 0)))))
    ck = rng.choice(3, (N, 8, 1, V), p=[0.5, 0.15, 0.35]); cap = np.where(ck == 0, 63, np.where(ck == 1, 0, 63 * rng.integers(0, 2, sh)))
    up = rng.random(sh) < rng.choice(np.array([0.0, 0.1, 0.2]), (N, 8, 1, V))
    B = np.where(up, W - 1, 0); T = np.where(up, 15, 0); K = np.where(up, 0, 15)
    fr = rng.random(sh) < rng.choice(np.array([0.0, 0.1, 0.2, 0.4]), (N, 8, 1, V)); live = rng.random(sh) < 0.8
    B = np.where(fr, np.where(rng.random(sh) < 0.7, rng.integers(0, W, sh), rng.choice(np.array([0, V - 1, V, W - 1]), sh)), B)
    T = np.where(fr, np.where(live, 15, 15 * rng.integers(0, 2, sh)), T); K = np.where(fr, np.where(live, 0, 15 * rng.integers(0, 2, sh)), K)
    for j, first, col, c in ((0, 15, V - 1, 63), (1, 15, V - 2, 63), (2, 14, W - 1, 0)):
        a = S * (Q - 1 - j)
        B[:, 7, :, a:a + S] = 0; T[:, 7, :, a:a + S] = 0; K[:, 7, :, a:a + S] = 15; cap[:, 7, :, a:a + S] = c
        B[:, 7, first:, a:a + S] = col; T[:, 7, first:, a:a + S] = 15; K[:, 7, first:, a:a + S] = 0
    wt = np.where(rng.random((N, 8, 16, 1)) < 0.8, 255 * rng.integers(0, 2, (N, 8, 16, 1)), rng.integers(0, 256, (N, 8, 16, 1))); wt[:, 7] = 255; wt[:, 0, 0] = 0
    ka = np.where(rng.random((N, 8, 16, 1)) < 0.8, (V - 1) * rng.integers(0, 2, (N, 8, 16, 1)), rng.integers(0, V, (N, 8, 16, 1)))
    ka[:, 7] = rng.integers(0, V, (N, 16, 1)); ka[:, 0, 0] = 0; ka[:, 0, 1] = V - 1; ka[:, 7, 15] = V - 1
    return pack(res, cap, B, T, K, wt, ka)
def setup_inputs_full(rng):
    res, cap, B, T, K, wt, ka = parts(rng); q = rng.permutation(N); i = np.arange(Q); lane = np.arange(16).reshape(16, 1)
    res[..., W - 16:] = np.where(lane < np.arange(16), 200, 0)
    a = q[0]; T[a, :, :, 0::S] = 0; T[a, :, :, 1::S] = 0; cap[a, :, :, 1::S] = 63
    odd = rng.permutation(8 * Q)[:2 * int(rng.integers(1, 100)) + 1]; k = rng.integers(0, 16, odd.size); g = odd // Q; v = S * (odd % Q)
    B[a, g, k, v] = W - 16 + rng.integers(6, 16, odd.size); T[a, g, k, v] = 15; K[a, g, k, v] = 0
    a = q[1]; hit = lane == rng.integers(0, 16, (8, 1, Q))
    B[a, :, :, 0::S] = np.where(hit, W - 16 + rng.integers(6, 16, (8, 1, Q)), B[a, :, :, 0::S]); T[a, :, :, 0::S] = np.where(hit, 15, T[a, :, :, 0::S]); K[a, :, :, 0::S] = np.where(hit, 0, K[a, :, :, 0::S])
    for a, s in ((q[0], 2), (q[1], 1)):
        five = rng.random((8, 1, Q)) < 0.6; hit = lane == rng.integers(0, 16, (8, 1, Q))
        B[a, :, :, s::S] = np.where(five & hit, W - 11, B[a, :, :, s::S]); K[a, :, :, s::S] = np.where(five & hit, 0, K[a, :, :, s::S])
        T[a, :, :, s::S] = np.where(five, np.where(hit, 15, 0), T[a, :, :, s::S])
    a = q[2]; T[a] = 15; K[a] = 0; B[a, 1::2] = rng.integers(V, W, (4, 16, V))
    for g in (0, 4):
        base = rng.integers(200, 249, 16); turn = (lane + rng.integers(0, 16, (1, Q - 16))) % 16
        res[a, g, :, W - Q:W - 16] = base[turn] + (lane < rng.integers(0, 8, (1, Q - 16)))
        B[a, g] = np.where(rng.random((1, V)) < 0.5, rng.integers(W - Q, W - 16, (16, V)), B[a, g])
    a = q[3]; r = (a + 1) % N; T[a, :, :, 0::S] = 0
    for g in range(8):
        x, y = rng.permutation(16)[:2]; wt[r, g] = 0; wt[r, g, x] = 16; wt[r, g, y] = 1
        if g != 3: ka[r, g] = int(ka[r, g, 0, 0])
        o = rng.permutation(4096); p = ((o * o >> 5) + int(ka[r, g, 0, 0]) * o) & (V - 1)
        first = rng.permutation(np.unique(p, return_index=True)[1]); n = (Q, 8, Q, 1, Q, 8, Q, 1)[g]
        s = (o[first[rng.permutation(Q) % n]] - 37 * i) & 4095; col = V + rng.permutation(Q); k = rng.integers(0, 16, Q)
        res[a, g, :, V:V + Q] = 0; res[a, g, x, col] = s >> 4; res[a, g, y, col] = s & 15
        B[a, g, k, S * i] = col; T[a, g, k, S * i] = 15; K[a, g, k, S * i] = 0
    return pack(res, cap, B, T, K, wt, ka)
def setup_inputs_spread(rng):
    res, cap, B, T, K, wt, ka = parts(rng)
    res = (np.exp2(8 * rng.random((N, 8, 1, W)) ** 3) * rng.random((N, 8, 16, W))).astype(np.int64)
    res = np.where(rng.random((N, 8, 1, W)) < 0.02, rng.integers(0, 256, res.shape), np.minimum(res, 255))
    cap = np.minimum((np.exp2(6 - 6 * rng.random((N, 8, 1, V)) ** 3) * rng.random(cap.shape)).astype(np.int64), 63)
    B = np.minimum((W * rng.random(B.shape) ** rng.choice(np.array([0.5, 1.0, 3.0]), (N, 8, 1, 1))).astype(np.int64), W - 1)
    wt = np.minimum(np.exp2(8 * rng.random(wt.shape)).astype(np.int64), 255)
    return pack(res, cap, B, T, K, wt, ka)
def setup_inputs_ties(rng):
    res, cap, B, T, K, wt, ka = parts(rng)
    lane = np.arange(16).reshape(16, 1); turn = (lane + rng.integers(0, 16, (N, 8, 1, W))) % 16
    res = np.where(turn < rng.integers(2, 4, (N, 8, 1, W)), 40, 0)
    cap = np.broadcast_to(rng.choice(np.array([0, 20, 20, 39, 40, 63]), (N, 8, 1, V)), cap.shape)
    live = rng.random(B.shape) < rng.choice(np.array([0.1, 0.2, 0.3]), (N, 8, 1, 1))
    T = np.where(live, 15, 0); K = np.where(live, 0, K)
    wt[:, ::2] = 1; ka[:, 1::2] = rng.choice(np.array([0, 1, V >> 1, V - 1]), (N, 4, 16, 1))
    return pack(res, cap, B, T, K, wt, ka)
def check_inputs(d):
    bad = []
    for k, lo, hi in (("res", 0, 255), ("cap", 0, 63), ("br", -983040, 63231), ("wt", 0, 255), ("ka", 0, V - 1)):
        v = np.asarray(d[k]).astype(np.float64)
        if not np.all((v >= lo) & (v <= hi) & (v == np.floor(v))): bad.append("range of " + k)
    if np.any((np.asarray(d["br"]).astype(np.int64) & 4095) >= W): bad.append("column numbers in br")
    return bad
def reference(res, cap, br, wt, ka):
    R = res.astype(np.float32).astype(np.int32).reshape(N, 8, 16, W); C = cap.astype(np.float32).astype(np.int32).reshape(N, 8, 16, V)
    b = np.array(br, dtype=np.int32).reshape(N, 8, 16, V); w = wt.astype(np.int64).reshape(N, 8, 16, 1); kf = ka.astype(np.int64).reshape(N, 8, 16, 1)
    A = [0] * N; row = np.arange(16).reshape(1, 16, 1); i = np.arange(Q)
    for t in range(1, RO + 1):
        v = S * i + (t - 1) % S; sent = []
        for r in range(N):
            x = b[r][:, :, v]; on = (((x >> 12) & 15) >= t) & (-(x >> 16) < t)
            c = C[r][:, :, v]; most = 4 + (A[r] & 1)
            pick = np.take_along_axis(R[r], (x & 4095).reshape(8, 1, 16 * Q), 2).reshape(8, 16, 16, Q) * on[:, None]
            m = np.max(pick, axis=2); fail = np.sum(m > c, axis=1) > most
            over = np.where(on, np.sum(np.maximum(pick - c[:, :, None], 0), axis=1), -1)
            gone = fail[:, None] & (row == np.argmax(over, axis=1)[:, None])
            m = np.max(pick * (~gone)[:, None], axis=2)
            m = np.where((np.sum(m > c, axis=1) > most)[:, None], 0, m)
            b[r][:, :, v] = np.where(gone, (x & 65535) - 65536 * (t + S), x)
            R[r][:, :, v] = m; A[r] = int(np.sum(fail)); sent.append(m)
        for r in range(N):
            m = sent[(r - 1 - (t - 1) % (N - 1)) % N]
            u = (np.sum(w[r] * m, axis=1) + 37 * i) & 4095
            p = ((u * u >> 5)[:, None] + kf[r] * u[:, None]) & (V - 1)
            slack = np.maximum(C[r] - R[r][:, :, :V], 0)
            sl = np.take_along_axis(slack, p.reshape(8, 1, 16 * Q), 2).reshape(8, 16, 16, Q)
            score = np.sum(np.minimum(m[:, :, None], sl), axis=1)
            par = np.take_along_axis(p, np.argmax(score, axis=1)[:, None], 1)[:, 0]
            for g in range(8):
                node, first = np.unique(par[g], return_index=True)
                b[r, g, first & 15, node] = V + Q * (t - 1) + first + 4096 * (t + 2)
            if t < RO: R[r][:, :, V + Q * (t - 1):V + Q * t] = m
    return {"yr": np.ascontiguousarray(R[..., :V]).reshape(N, 128, V).astype(np.float32).astype(BF), "yb": b.reshape(N, 128, V).astype(np.float32)}

@@ -1,0 +1,649 @@
+import numpy as np
+from concourse.mybir import dt, AluOpType as A, AxisListType, ActivationFunctionType as F
+
+NR, NQ, ZC = 4, 256, 1792
+SM = 5
+EARLY = 5
+SA = 4
+HS = 128
+BIG = float(2 ** 25)
+
+SCRATCH = {
+    "resw": ("sbuf", [128, 1808], "bfloat16"),
+    "capb": ("sbuf", [128, 1024], "bfloat16"),
+    "slack": ("sbuf", [128, 1024], "bfloat16"),
+    "bri": ("sbuf", [128, 1024], "int32"),
+    "words": ("sbuf", [128, 1280], "float32"),
+    "pick": ("sbuf", [128, 4352], "bfloat16"), "over": ("sbuf", [128, 4352], "bfloat16"),
+    "scn": ("sbuf", [128, 4096], "bfloat16"), "mins": ("sbuf", [128, 4096], "bfloat16"),
+    "slg": ("sbuf", [128, 4096], "bfloat16"), "key": ("sbuf", [128, 16, 32], "float32"),
+    "eq": ("sbuf", [128, 2560], "bfloat16"), "fs": ("sbuf", [128, 2560], "float16"),
+    "seg": ("sbuf", [128, 2048], "bfloat16"), "inc": ("sbuf", [128, 2560], "bfloat16"), "uq": ("sbuf", [128, 2, 256], "int32"),
+}
+
+
+PART = {}
+
+
+def declare(names, cols, dtype, pool=None):
+    for j, nm in enumerate(names.split()):
+        if pool is None:
+            SCRATCH[nm] = ("sbuf", [128, cols], dtype)
+        else:
+            SCRATCH[pool] = ("sbuf", [128, cols * (j + 1)], dtype)
+            PART[nm] = (pool, cols * j, cols * (j + 1))
+
+
+declare("wti kai ai aj", 1, "int32")
+declare("wtf kaf asum", 1, "float32")
+declare("kt ksc", 512, "float32")
+declare("seg32", 512, "bfloat16")
+declare("z1 z4k z256 nz256 wz", 144, "bfloat16")
+declare("idn nidn ones bon", 128, "bfloat16")
+declare("bonh", 128, "float16")
+declare("bonf nidf iom ion", 128, "float32")
+declare("dm nd posk kc10 kc11 kc30 kc31 loc ngb xw ptf pts", 256, "float32")
+declare("ioa iob ioc iod ioe iof dwb", 256, "float32", "iox")
+declare("kr ptx parh", 256, "float16")
+declare("zero k0 sg g2 dc dr", 256, "bfloat16")
+declare("lo lo2 bb xi xi2 oo t2 pl", 256, "int32")
+declare("lst pu", 256, "uint16")
+declare("cl posu ku fixu paru wlu", 16, "uint16")
+declare("expct posf npt win", 16, "float32")
+declare("dump wdump c37 dumpf kk onn ps4 de de2 f1 f2 wd w1 w2", 16, "float32", "tin")
+declare("fail", 16, "bfloat16")
+declare("ki kj x16 sq pi r3", 16, "int32")
+declare("bg", 8, "bfloat16")
+declare("iog", 8, "float32")
+declare("pcol", 16, "float32")
+declare("pi0", 4, "int32")
+declare("bt", 4, "float32")
+declare("lim", 2, "float32")
+declare("io16", 80, "float32")
+declare("dw1 dw2 dw3 dw4", 256, "float32")
+declare("send1 send2 send3 send4 land1 land2 land3 land4", 256, "bfloat16")
+PSB = ("psS", "psC", "psU", "psK", "psB0", "psB1", "psG", "psX")
+for _n in PSB:
+    SCRATCH[_n] = ("psum", [128, 512], "float32")
+SEMAPHORES = ["qv", "qp", "qs", "qg", "snt"] + ["d%d" % k for k in range(8)] + ["arr%d" % k for k in range(1, NR + 1)]
+QSEM = {"V": "qv", "P": "qp", "S": "qs", "G": "qg"}
+CACHE = {}
+
+
+def R(name, *idx):
+    return ("ap", name, idx)
+
+
+def C(name, a, b, st=1):
+    return ("ap", name, (slice(a, b, st),))
+
+
+def ALL(name):
+    return C(*PART[name]) if name in PART else ("ap", name, ())
+
+
+def IND(win, off):
+    return ("ind", win, off)
+
+
+def cols_of(x):
+    shp = SCRATCH[x[1]][1][1:]
+    n = int(np.prod(shp))
+    return n, np.arange(n).reshape(shp)[x[2]].ravel()
+
+
+def size(x):
+    return size(x[2]) * 16 if x[0] == "ind" else cols_of(x)[1].size
+
+
+def build():
+    ops = []
+
+    def add(q, m, args, kw, reads, writes, dur, grp=None):
+        ops.append({"q": q, "m": m, "args": args, "kw": kw, "r": reads, "w": writes, "dur": dur, "grp": grp, "tag": m})
+
+    def split(out, ins):
+        rd, wr = [], []
+        for x in ins:
+            if isinstance(x, tuple):
+                rd += [x[1], x[2]] if x[0] == "ind" else [x]
+        if out[0] == "ind":
+            rd.append(out[2])
+            wr.append(out[1])
+        else:
+            wr.append(out)
+        return rd, wr
+
+    def V(m, out, *ins, **kw):
+        rd, wr = split(out, ins)
+        n = size(out)
+        if m == "tensor_tensor":
+            cyc = n if any(x[1] in PSB for x in ins[:2]) else 2 * n
+        elif m == "tensor_reduce":
+            cyc = size(ins[0])
+        else:
+            wide = [x for x in (out,) + ins if isinstance(x, tuple) and x[0] == "ap" and size(x) > 1 and SCRATCH[x[1]][2] in ("float32", "int32")]
+            cyc = n if wide else n / 2
+        if out[0] == "ind":
+            cyc = 3.0 * n
+        if any(isinstance(x, tuple) and x[0] == "ind" for x in ins):
+            cyc = 1.56 * n
+        add("V", m, (out,) + ins, kw, rd, wr, 60 + 1.04 * max(cyc, 64))
+
+    def TT(out, a, b, op):
+        V("tensor_tensor", out, a, b, op)
+
+    def TS(out, a, s1, op0, s2=None, op1=None):
+        if op1 is None:
+            V("tensor_scalar", out, a, s1, None, op0)
+        else:
+            V("tensor_scalar", out, a, s1, s2, op0, op1)
+
+    def CP(out, a):
+        V("tensor_copy", out, a)
+
+    def MS(out, val):
+        V("memset", out, val)
+
+    def SCAN(out, d0, d1, o0, o1):
+        V("tensor_tensor_scan", out, d0, d1, 0.0, o0, o1)
+
+    def S(out, a, func, after=(), **kw):
+        rd, wr = split(out, [a] + list(kw.values()))
+        c = 1.56 * size(a) if a[0] == "ind" else size(a)
+        add("S", "activation", (out, a, func), kw, rd, wr, 65 + 1.04 * max(c, 64))
+        if after:
+            ops[-1]["after"] = after
+
+    def SI(out, a, **kw):
+        S(out, a, F.Identity, **kw)
+
+    ng = [0]
+
+    def group():
+        ng[0] += 1
+        return ng[0]
+
+    def MM(out, l, r, grp):
+        f4 = 4 if SCRATCH[r[1]][2] == "float32" else 1
+        add("P", "matmul", (out, l, r), {}, [l, r], [out], 10 + f4 * max(64, size(r)) * 0.5, grp)
+
+    def IOTA(out, pattern, base, cm):
+        kw = {} if SCRATCH[out[1]][2] == "int32" else {"allow_small_or_imprecise_dtypes": True}
+        add("G", "iota", (out, pattern, base, cm), kw, [], [out], 130 + 2 * size(out))
+
+    nd = [0]
+
+    def DMA(q, out, in_, dur):
+        add(q, "dma_start", (out, in_), {}, [in_] if in_[1] in SCRATCH else [], [out] if out[1] in SCRATCH else [], dur)
+        ops[-1]["sem"] = "d%d" % nd[0]
+        nd[0] += 1
+
+    def cset(n, s):
+        return C(n, s - 1, 1024, 4)
+
+    DMA("Y", ALL("bri"), ALL("br"), 4000)
+    DMA("Y", C("resw", 0, ZC), ALL("res"), 4500)
+    DMA("S", ALL("capb"), ALL("cap"), 4000)
+    DMA("S", ALL("kai"), ALL("ka"), 2000)
+    DMA("S", ALL("wti"), ALL("wt"), 2000)
+    p0 = C("pi0", 0, 1)
+
+    def pc(j):
+        return C("pcol", j, j + 1)
+    IOTA(p0, [[0, 1]], 0, 1)
+    IOTA(ALL("iog"), [[1, 8]], 0, 0)
+    IOTA(ALL("iom"), [[1, 128]], 0, 0)
+    IOTA(ALL("ion"), [[1, 8], [0, 16]], 0, 0)
+    IOTA(ALL("iob"), [[-15, 256]], 4095, 0)
+    IOTA(C("io16", 0, 16), [[16, 16]], 4096, 0)
+    IOTA(C("io16", 16, 32), [[592, 16]], 0, 0)
+    IOTA(C("io16", 32, 48), [[0, 4], [16, 4]], -63, 0)
+    IOTA(C("io16", 48, 64), [[16, 16]], 1024, 0)
+    IOTA(C("io16", 64, 80), [[1, 16]], 0, 0)
+    IOTA(ALL("ioa"), [[1, 16], [0, 16]], -15, 0)
+    IOTA(ALL("ioc"), [[0, 16], [1, 16]], 0, 0)
+    IOTA(ALL("iod"), [[1, 16], [0, 16]], 240, 0)
+    IOTA(ALL("ioe"), [[16, 256]], 0, 0)
+    MS(C("resw", ZC, ZC + 16), 0.0)
+    MS(ALL("seg"), 1.0)
+    MS(C("seg", 0, 2048, 16), 0.0)
+    MS(ALL("z1"), 0.0)
+    TS(C("pi0", 1, 2), p0, 15, A.bitwise_and)
+    TS(C("pi0", 2, 3), p0, 4, A.arith_shift_right)
+    TS(C("pi0", 3, 4), C("pi0", 2, 3), 1, A.bitwise_and)
+    CP(pc(0), p0)
+    CP(C("pcol", 1, 4), C("pi0", 1, 4))
+    pb, pg, ph = pc(1), pc(2), pc(3)
+    TS(pc(4), ph, 0.0, A.is_equal, -BIG, A.mult)
+    TS(pc(5), ph, 1.0, A.is_equal, -BIG, A.mult)
+    TS(pc(6), pb, -1.0, A.mult)
+    TS(pc(7), pb, 16.0, A.mult)
+    TS(ALL("bg"), ALL("iog"), pg, A.is_equal)
+    CP(C("z1", 15, 143, 16), ALL("bg"))
+    TS(ALL("idn"), ALL("iom"), pc(0), A.is_equal)
+    SI(ALL("nidn"), ALL("idn"), scale=-1.0)
+    TT(pc(8), pc(5), pb, A.subtract)
+    TT(pc(9), pc(4), pb, A.subtract)
+    TT(pc(10), pc(5), pc(7), A.subtract)
+    TT(pc(11), pc(4), pc(7), A.subtract)
+    x = cset("bri", 1)
+    TS(ALL("bb"), x, 4095, A.bitwise_and)
+    TS(ALL("k0"), x, 4096.0, A.is_lt, float(ZC), A.mult)
+    TT(ALL("oo"), ALL("bb"), ALL("k0"), A.max)
+    CP(ALL("lst"), ALL("oo"))
+    SI(ALL("z4k"), ALL("z1"), scale=4096.0)
+    for h in range(2):
+        SI(ALL("kc1%d" % h), ALL("iob"), bias=pc(8 + h))
+        SI(ALL("kc3%d" % h), ALL("iod"), bias=pc(10 + h))
+    MS(ALL("seg32"), 1.0)
+    MS(C("seg32", 0, 512, 32), 0.0)
+    MS(ALL("zero"), 0.0)
+    MS(C("lim", 0, 1), 4.0)
+    MS(C("lim", 1, 2), 8.0)
+    SI(ALL("dump"), C("io16", 0, 16), bias=pb)
+    TS(ALL("bon"), ALL("ion"), pg, A.is_equal)
+    CP(ALL("bonh"), ALL("bon"))
+    CP(ALL("kaf"), ALL("kai"))
+    CP(ALL("wtf"), ALL("wti"))
+    SI(ALL("wz"), ALL("z1"), scale=ALL("wtf"))
+    TS(ALL("kr"), ALL("ioa"), pc(6), A.is_equal, ALL("kaf"), A.mult)
+    MM(C("psK", 0, 256), ALL("bonh"), ALL("kr"), group())
+    for t in range(1, NR):
+        SI(C("bt", t, t + 1), pb, bias=-4.0 * t)
+    SI(pc(12), pb, scale=37.0)
+    SI(ALL("c37"), C("io16", 16, 32), bias=pc(12))
+    SI(ALL("z256"), ALL("z1"), scale=256.0)
+    SI(ALL("nz256"), ALL("z1"), scale=-256.0)
+    TS(ALL("dm"), ALL("ioc"), pb, A.is_equal)
+    SI(ALL("expct"), C("io16", 32, 48), bias=pb)
+    SI(C("inc", 0, 2048), ALL("seg"), scale=0.0, bias=-1.0)
+    SI(C("inc", 2048, 2560), C("seg", 0, 512), scale=0.0, bias=-1.0)
+    o = 0
+    for qd in range(4):
+        L = 64 * (qd + 1)
+        SI(C("inc", o, o + 4 * L, L), C("seg", 0, 4), scale=0.0, bias=1024.0)
+        o += 4 * L
+    SI(ALL("wdump"), C("io16", 48, 64), bias=pb)
+    CP(ALL("cl"), C("io16", 64, 80))
+    SI(ALL("bonf"), ALL("bon"))
+    SI(ALL("ones"), C("seg", 0, 128), scale=0.0, bias=1.0)
+    SI(ALL("posk"), ALL("ioe"), bias=pb)
+    SI(ALL("nidf"), ALL("idn"), scale=-1.0)
+    SI(ALL("nd"), ALL("dm"), scale=-1.0, bias=1.0)
+    CP(C("words", 0, 1024), ALL("bri"))
+    IOTA(ALL("iof"), [[1, 256]], -2 ** 20, 0)
+    SI(ALL("xw"), ALL("dm"), scale=float(2 ** 20))
+    TT(ALL("dwb"), ALL("xw"), ALL("iof"), A.add)
+    for t in range(1, NR + 1):
+        S(ALL("dw%d" % t), ALL("dwb"), F.Relu, bias=1024.0 + 256 * (t - 1) + 4096 * (t + 2))
+
+    def background(t, share=()):
+        for c in range(8):
+            out, win = C("pick", 512 * c, 512 * c + 512), IND(C("resw", 0, 1808), C("lst", 32 * c, 32 * c + 32))
+            if t == 1 and c % 2:
+                CP(out, win)
+            else:
+                S(out, win, F.Copy, after=share if c >= EARLY else ())
+        for q in range(8):
+            bank = (("psB0", "psB1") if t > 1 else ("psB0", "psB1", "psC", "psU"))[q % (2 if t > 1 else 4)]
+            for j in range(2):
+                gr = group()
+                MM(C(bank, 256 * j, 256 * j + 256), ALL("idn"), C("pick", 2 * q + j, 4096, 16), gr)
+                MM(C(bank, 256 * j, 256 * j + 256), ALL("nidn"), cset("capb", t), gr)
+            for j in range(2):
+                out, src = C("over", 2 * q + j, 4096, 16), C(bank, 256 * j, 256 * j + 256)
+                if t == 1 and q % 2:
+                    TS(out, src, 0.0, A.max)
+                else:
+                    S(out, src, F.Relu)
+
+    def argmax(src, kc):
+        for h in range(2):
+            TT(R("key", slice(None), slice(16 * h, 16 * h + 16)), src, ALL(kc + "%d" % h), A.add)
+        V("transpose", ALL("kt"), ALL("key"))
+        SCAN(ALL("ksc"), ALL("seg32"), ALL("kt"), A.mult, A.max)
+        CP(ALL("ki"), C("ksc", 31, 512, 32))
+
+    def step1(t):
+        n1 = 16 * HS
+        for a in range(0, n1, 2048):
+            w = min(2048, n1 - a)
+            SCAN(C("scn", a, a + w), C("seg", 0, w), C("pick", a, a + w), A.mult, A.max)
+        gr = group()
+        for k in range(16):
+            MM(C("psS", 0, 256), C("z4k", 15 - k, 143 - k), C("over", k, 4096, 16), gr)
+        if HS < NQ:
+            gr = group()
+            for k in range(16):
+                MM(C("psG", HS, NQ), ALL("idn"), C("over", n1 + k, 4096, 16), gr)
+        gr = group()
+        MM(C("psG", 0, HS), ALL("idn"), C("scn", 15, n1, 16), gr)
+        MM(C("psG", 0, HS), ALL("nidn"), C("capb", t - 1, 4 * HS, 4), gr)
+        S(ALL("sg"), C("psG", 0, 256), F.Sign, bias=-0.5)
+        gr = group()
+        for b in range(16):
+            MM(C("psU", 16, 32), C("z1", 15 - b, 143 - b), C("sg", b, 256, 16), gr)
+        argmax(C("psS", 0, 256), "kc1")
+        TS(ALL("kj"), ALL("ki"), 4095, A.bitwise_and)
+        TS(ALL("fail"), C("psU", 16, 32), C("lim", 1, 2), A.add, 0.0, A.is_gt)
+        TT(ALL("dumpf"), ALL("dump"), ALL("fail"), A.subtract)
+        TT(ALL("kk"), ALL("kj"), ALL("fail"), A.mult)
+        TT(ALL("posf"), ALL("dumpf"), ALL("kk"), A.subtract)
+        CP(ALL("posu"), ALL("posf"))
+        V("tensor_copy", IND(C("pick", 0, 4352), ALL("posu")), ALL("zero"))
+        for a in (0, 2048):
+            SCAN(C("scn", a, a + 2048), ALL("seg"), C("pick", a, a + 2048), A.mult, A.max)
+        m = C("scn", 15, 4096, 16)
+        MM(C("psS", 256, 512), ALL("idn"), cset("capb", t), group())
+        TT(ALL("g2"), m, C("psS", 256, 512), A.is_gt)
+        MM(C("psX", 0, 256), ALL("bon"), ALL("g2"), group())
+        TS(C("psX", 256, 512), C("psX", 0, 256), C("lim", 0, 1), A.is_le)
+        sn = ALL("send%d" % t)
+        TT(sn, m, C("psX", 256, 512), A.mult)
+        add("G", "remote", (t,), {}, [sn], [], 1500)
+        S(cset("resw", t), sn, F.Copy)
+        gr = group()
+        MM(C("psG", 256, 512), ALL("idn"), cset("capb", t), gr)
+        MM(C("psG", 256, 512), ALL("nidn"), sn, gr)
+        S(cset("slack", t), C("psG", 256, 512), F.Relu)
+        if t == NR:
+            DMA("Y", ALL("yr"), C("resw", 0, 1024), 3500)
+        else:
+            MM(C("psU", 32, 48), ALL("ones"), ALL("fail"), group())
+            V("tensor_reduce", ALL("asum"), C("psU", 32, 48), AxisListType.X, A.add)
+            CP(ALL("ai"), ALL("asum"))
+            TS(ALL("aj"), ALL("ai"), 1, A.bitwise_and)
+            TS(C("lim", 0, 1), ALL("aj"), 4.0, A.add)
+            TS(C("lim", 1, 2), ALL("aj"), -2.0, A.mult, 8.0, A.add)
+
+    def merge(t):
+        TT(ALL("w1"), ALL("win"), ALL("wd"), A.mult)
+        TT(ALL("w2"), ALL("w1"), ALL("wdump"), A.add)
+        CP(ALL("wlu"), ALL("w2"))
+        TT(ALL("xw"), IND(C("words", 0, 1024), ALL("paru")), ALL("nd"), A.mult)
+        TT(IND(C("words", 0, 1280), ALL("wlu")), ALL("xw"), ALL("dw%d" % t), A.add)
+
+    def suspend(t):
+        TT(ALL("ptf"), IND(ALL("posf"), ALL("cl")), ALL("dm"), A.mult)
+        gr = group()
+        MM(C("psX", 0, 256), ALL("bonf"), ALL("ptf"), gr)
+        MM(C("psX", 0, 256), ALL("nidf"), ALL("posk"), gr)
+        CP(ALL("xi"), cset("words", t))
+        TS(ALL("lo"), ALL("xi"), 65535, A.bitwise_and)
+        S(ALL("ngb"), C("psX", 0, 256), F.Square, scale=2048.0)
+        S(C("psC", 0, 256), ALL("ngb"), F.Identity, bias=-65536.0 * (t + 4))
+        TT(C("psC", 256, 512), ALL("lo"), C("psC", 0, 256), A.add)
+        TT(cset("words", t), cset("words", t), C("psC", 256, 512), A.min)
+
+    def makelist(s):
+        x = cset("bri", 2)
+        if s > 2:
+            x = ALL("xi2")
+            CP(x, cset("words", s))
+        S(ALL("loc"), cset("words", s), F.Relu, scale=-2048.0, bias=-2048.0 * 65536.0 * (s - 1))
+        TS(ALL("lo2"), x, 65535, A.bitwise_and)
+        TS(ALL("bb"), x, 4095, A.bitwise_and)
+        TS(C("psS", 0, 256), ALL("lo2"), 4096.0 * s, A.is_lt, float(ZC), A.mult)
+        TT(C("psS", 256, 512), C("psS", 0, 256), ALL("loc"), A.max)
+        TT(ALL("oo"), C("psS", 256, 512), ALL("bb"), A.max)
+        TS(ALL("lst"), ALL("oo"), float(ZC), A.min)
+
+    def step3(t):
+        ln = "land%d" % t
+        la = ALL(ln)
+        add("arr", "arr", (t,), {}, [], [la], 3500)
+        gr = group()
+        for b in range(16):
+            MM(C("psU", 0, 16), C("wz", 15 - b, 143 - b), C(ln, b, 256, 16), gr)
+        TT(ALL("x16"), C("psU", 0, 16), ALL("c37"), A.add)
+        u16 = R("uq", 0, slice(0, 16))
+        TS(u16, ALL("x16"), 4095, A.bitwise_and)
+        TT(ALL("sq"), u16, u16, A.mult)
+        TS(R("uq", 1, slice(0, 16)), ALL("sq"), 5, A.arith_shift_right)
+        for w in (16, 32, 64, 128):
+            CP(R("uq", slice(None), slice(w, 2 * w)), R("uq", slice(None), slice(0, w)))
+        TT(C("psK", 256, 512), R("uq", 0, slice(0, 256)), C("psK", 0, 256), A.mult)
+        TT(ALL("t2"), C("psK", 256, 512), R("uq", 1, slice(0, 256)), A.add)
+        TS(ALL("pl"), ALL("t2"), 1023, A.bitwise_and)
+        CP(ALL("pu"), ALL("pl"))
+        gr = group()
+        nv = 16 - SM
+        share = []
+        for m in range(nv, 16):
+            S(C("slg", 256 * m, 256 * m + 256), IND(ALL("slack"), C("pu", 16 * m, 16 * m + 16)), F.Copy)
+            share.append(len(ops) - 1)
+        for m in range(nv):
+            TT(C("mins", 256 * m, 256 * m + 256), IND(ALL("slack"), C("pu", 16 * m, 16 * m + 16)), la, A.min)
+            MM(C("psC", 0, 256), C("z256", m, m + 128), C("mins", 256 * m, 256 * m + 256), gr)
+        for m in range(nv, 16):
+            h = 256 * (m % 2)
+            bank = "psG" if m % 2 else "psS"
+            g2 = group()
+            MM(C(bank, h, h + 256), ALL("idn"), la, g2)
+            MM(C(bank, h, h + 256), ALL("nidn"), C("slg", 256 * m, 256 * m + 256), g2)
+            MM(C("psC", 0, 256), C("z256", m, m + 128), la, gr)
+            S(C("mins", 256 * m, 256 * m + 256), C(bank, h, h + 256), F.Relu)
+            share.append(len(ops) - 1)
+            MM(C("psC", 0, 256), C("nz256", m, m + 128), C("mins", 256 * m, 256 * m + 256), gr)
+        argmax(C("psC", 0, 256), "kc3")
+        TS(ALL("kj"), ALL("ki"), 255, A.bitwise_and)
+        CP(ALL("ku"), ALL("kj"))
+        TT(ALL("ptx"), IND(ALL("pl"), ALL("ku")), ALL("dm"), A.mult)
+        MM(C("psX", 0, 256), ALL("bonh"), ALL("ptx"), group())
+        SCAN(ALL("pts"), C("seg", 0, 256), ALL("ptx"), A.mult, A.add)
+        pt = C("pts", 15, 256, 16)
+        CP(ALL("parh"), C("psX", 0, 256))
+        SI(ALL("npt"), pt, scale=-1024.0)
+        o = 0
+        for a in range(16):
+            L = 64 * (a // 4 + 1)
+            if a >= 16 - SA:
+                S(C("eq", o, o + L), C("psX", 0, L), F.Abs, scale=1024.0, bias=C("npt", a, a + 1))
+            else:
+                TS(C("eq", o, o + L), C("parh", 0, L), C("pts", 16 * a + 15, 16 * a + 16), A.not_equal, 1024.0, A.mult)
+            o += L
+        SCAN(ALL("fs"), ALL("inc"), ALL("eq"), A.add, A.min)
+        CP(ALL("pi"), pt)
+        CP(ALL("paru"), pt)
+        if t < NR:
+            TT(ALL("dc"), IND(ALL("capb"), ALL("paru")), la, A.subtract)
+            S(ALL("dr"), ALL("dc"), F.Relu, scale=-1.0)
+            TS(ALL("r3"), ALL("pi"), 3, A.bitwise_and)
+            TS(ALL("onn"), ALL("r3"), float(t), A.is_equal)
+            SI(ALL("ps4"), pt, scale=4.0, bias=C("bt", t, t + 1))
+            TT(ALL("de"), ALL("ps4"), ALL("dump"), A.subtract)
+            TT(ALL("de2"), ALL("de"), ALL("onn"), A.mult)
+        TT(ALL("wd"), ALL("pi"), ALL("wdump"), A.subtract)
+        o = 0
+        for qd in range(4):
+            L = 64 * (qd + 1)
+            TT(C("win", 4 * qd, 4 * qd + 4), C("fs", o + L - 1, o + 4 * L, L), C("expct", 4 * qd, 4 * qd + 4), A.is_equal)
+            o += 4 * L
+        if t < NR:
+            S(C("resw", 1024 + 256 * (t - 1), 1280 + 256 * (t - 1)), la, F.Copy)
+            background(t + 1, share)
+            TT(ALL("f1"), ALL("win"), ALL("de2"), A.mult)
+            TT(ALL("f2"), ALL("f1"), ALL("dump"), A.add)
+            CP(ALL("fixu"), ALL("f2"))
+            V("tensor_copy", IND(C("over", 0, 4352), ALL("fixu")), ALL("dr"))
+            V("tensor_copy", IND(C("pick", 0, 4352), ALL("fixu")), la)
+
+    background(1)
+    for c in range(2):
+        gr = group()
+        MM(C("psX", 0, 512), ALL("idn"), C("capb", 512 * c, 512 * c + 512), gr)
+        MM(C("psX", 0, 512), ALL("nidn"), C("resw", 512 * c, 512 * c + 512), gr)
+        S(C("slack", 512 * c, 512 * c + 512), C("psX", 0, 512), F.Relu)
+    for t in range(1, NR + 1):
+        step1(t)
+        if t > 1:
+            merge(t - 1)
+        suspend(t)
+        if t < NR:
+            makelist(t + 1)
+        step3(t)
+    merge(NR)
+    DMA("Y", ALL("yb"), C("words", 0, 1024), 4500)
+    return ops
+
+
+LAT = 90
+
+
+def depend(ops):
+    hist, deps, order, sends = {}, [], [], {}
+    for i, op in enumerate(ops):
+        dp, od, acc = set(), set(op.get("after", ())), []
+        for w, lst in ((0, op["r"]), (1, op["w"])):
+            for x in lst:
+                n, cs = cols_of(x)
+                m = np.zeros(n, bool)
+                m[cs] = True
+                acc.append((w, x[1], m))
+        for w, nm, m in acc:
+            ps = nm in PSB
+            for (j, w2, m2) in hist.get(nm, ()):
+                o2 = ops[j]
+                if ps and op["q"] == "P" and o2["q"] == "P":
+                    if o2["grp"] != op["grp"]:
+                        od.add(j)
+                elif ps and o2["q"] != op["q"]:
+                    dp.add(j)
+                elif (w or w2) and bool(np.any(m & m2)):
+                    dp.add(j)
+        for w, nm, m in acc:
+            h = hist.setdefault(nm, [])
+            if nm in PSB:
+                h[:] = h[-140:]
+            elif w:
+                h[:] = [e for e in h if bool(np.any(e[2] & ~m))]
+            h.append((i, w, m))
+        if op["m"] == "remote":
+            sends[op["args"][0]] = i
+        if op["m"] == "arr":
+            od.add(sends[op["args"][0]])
+        dp.discard(i)
+        deps.append(dp)
+        order.append(od - dp)
+    return deps, order
+
+
+def schedule(ops, deps, order):
+    n = len(ops)
+    pre = [deps[i] | order[i] for i in range(n)]
+    nxt = [[] for _ in range(n)]
+    for i in range(n):
+        for j in pre[i]:
+            nxt[j].append(i)
+    prio = [0.0] * n
+    for i in range(n - 1, -1, -1):
+        prio[i] = ops[i]["dur"] + LAT + max([prio[k] for k in nxt[i]] + [0.0])
+    left = [len(p) for p in pre]
+    ready, est, free, out = {}, [0.0] * n, {}, []
+    fin, start = [0.0] * n, [0.0] * n
+    for i in range(n):
+        if not left[i]:
+            ready.setdefault(ops[i]["q"], []).append(i)
+    while len(out) < n:
+        best = None
+        for q, lst in ready.items():
+            if not lst:
+                continue
+            f = 0.0 if q == "arr" else free.get(q, 0.0)
+            e = min(max(f, est[i]) for i in lst)
+            c = max((i for i in lst if max(f, est[i]) <= e + 250), key=lambda i: prio[i])
+            if best is None or max(f, est[c]) < best[0]:
+                best = (max(f, est[c]), q, c)
+        s, q, c = best
+        ready[q].remove(c)
+        start[c], fin[c] = s, s + ops[c]["dur"]
+        free[q] = s + 100 if ops[c]["m"] == "dma_start" else fin[c]
+        out.append(c)
+        for k in nxt[c]:
+            left[k] -= 1
+            est[k] = max(est[k], fin[c] + (LAT if c in deps[k] or ops[k]["m"] == "arr" else 0))
+            if not left[k]:
+                ready.setdefault(ops[k]["q"], []).append(k)
+    return out, start, fin
+
+
+def rank_program(g, core, T, topo):
+    rank = T.rank_of(core)
+    if rank is None:
+        return
+    if "plan" not in CACHE:
+        ops = build()
+        deps, order = depend(ops)
+        seq, start, fin = schedule(ops, deps, order)
+        first, last = {}, {}
+        for i in seq:
+            gr = ops[i]["grp"]
+            if gr is not None:
+                first.setdefault(gr, i)
+                last[gr] = i
+        CACHE["plan"] = (ops, deps, seq, first, last)
+    ops, deps, seq, first, last = CACHE["plan"]
+    queues = {"V": g.vector, "P": g.tensor, "S": g.scalar, "G": g, "Y": g.sync}
+    call = {"tensor_tensor": g.vector.tensor_tensor, "tensor_scalar": g.vector.tensor_scalar, "tensor_copy": g.vector.tensor_copy,
+            "memset": g.vector.memset, "tensor_tensor_scan": g.vector.tensor_tensor_scan, "transpose": g.vector.transpose,
+            "tensor_reduce": g.vector.tensor_reduce, "activation": g.scalar.activation, "iota": g.iota}
+    n = len(T.cores)
+
+    def res(x):
+        if not isinstance(x, tuple):
+            return x
+        if x[0] == "ind":
+            return res(x[1]).indirect(res(x[2]))
+        return T[x[1]][(slice(None),) + x[2]]
+
+    count, known, comp, clk, total = {}, {}, {}, {}, {}
+    for i in seq:
+        op = ops[i]
+        q, m = op["q"], op["m"]
+        if q == "arr":
+            t = op["args"][0]
+            k = len(topo.engines(T.cores[(rank - 1 - (t - 1) % (n - 1)) % n], core))
+            comp[i], clk[i], total["arr%d" % t] = ("arr%d" % t, k), {}, k
+            continue
+        kn = known.setdefault(q, {})
+        need = {}
+        for d in deps[i]:
+            s, v = comp[d]
+            if kn.get(s, 0) < v and need.get(s, (0, 0))[0] < v:
+                need[s] = (v, d)
+        for s in sorted(need):
+            v, d = need[s]
+            if not any(s2 != s and clk[d2].get(s, 0) >= v for s2, (v2, d2) in need.items()):
+                queues[q].wait_ge(T.sem[s], v)
+        for s, (v, d) in need.items():
+            for s2, v2 in list(clk[d].items()) + [(s, v)]:
+                if kn.get(s2, 0) < v2:
+                    kn[s2] = v2
+        clk[i] = dict(kn)
+        if m == "remote":
+            t = op["args"][0]
+            dst = T.cores[(rank + 1 + (t - 1) % (n - 1)) % n]
+            rid, pid = topo.addr(dst, core)
+            g.remote_dma(out_ap=T["land%d" % t][:], in_ap=T["send%d" % t][:], remote_sem=T.sem["arr%d" % t], local_sem=T.sem.snt,
+                         pid=pid, routing_id=rid, dma_engine_mask=topo.mask(core, dst))
+            total["snt"] = total.get("snt", 0) + len(topo.engines(core, dst))
+            comp[i] = ("snt", 10 ** 6)
+            continue
+        args = [res(x) for x in op["args"]]
+        if m == "dma_start":
+            s = op["sem"]
+            queues[q].dma_start(args[0], args[1]).then_inc(T.sem[s], 16)
+            comp[i], total[s] = (s, 16), 16
+            continue
+        if m == "matmul":
+            gr = op["grp"]
+            c = g.tensor.matmul(args[0], args[1], args[2], first[gr] == i, last[gr] == i)
+        else:
+            c = call[m](*args, **{k: res(v) for k, v in op["kw"].items()})
+        s = QSEM[q]
+        count[q] = count.get(q, 0) + 1
+        c.then_inc(T.sem[s], 1)
+        comp[i], total[s] = (s, count[q]), count[q]
+    for s in sorted(total):
+        g.sync.wait_ge(T.sem[s], total[s])

@@ -2,11 +2,12 @@ import numpy as np
 from concourse.mybir import dt, AluOpType as A, AxisListType, ActivationFunctionType as F
 
 NR, NQ, ZC = 4, 256, 1792
-SM = 5
+SM = 4
+HALF = 2
 EARLY = 5
-SA = 4
-HS = 128
-BIG = float(2 ** 25)
+SA = 5
+SML, SAL = 6, 5
+HS = 256
 
 SCRATCH = {
     "resw": ("sbuf", [128, 1808], "bfloat16"),
@@ -16,9 +17,9 @@ SCRATCH = {
     "words": ("sbuf", [128, 1280], "float32"),
     "pick": ("sbuf", [128, 4352], "bfloat16"), "over": ("sbuf", [128, 4352], "bfloat16"),
     "scn": ("sbuf", [128, 4096], "bfloat16"), "mins": ("sbuf", [128, 4096], "bfloat16"),
-    "slg": ("sbuf", [128, 4096], "bfloat16"), "key": ("sbuf", [128, 16, 32], "float32"),
+    "slg": ("sbuf", [128, 4096], "bfloat16"),
     "eq": ("sbuf", [128, 2560], "bfloat16"), "fs": ("sbuf", [128, 2560], "float16"),
-    "seg": ("sbuf", [128, 2048], "bfloat16"), "inc": ("sbuf", [128, 2560], "bfloat16"), "uq": ("sbuf", [128, 2, 256], "int32"),
+    "seg": ("sbuf", [128, 2048], "bfloat16"), "inc": ("sbuf", [128, 2560], "bfloat16"),
 }
 
 
@@ -36,19 +37,21 @@ def declare(names, cols, dtype, pool=None):
 
 declare("wti kai ai aj", 1, "int32")
 declare("wtf kaf asum", 1, "float32")
-declare("kt ksc", 512, "float32")
-declare("seg32", 512, "bfloat16")
+declare("to00 to01 to10 to11", 128, "float32")
 declare("z1 z4k z256 nz256 wz", 144, "bfloat16")
 declare("idn nidn ones bon", 128, "bfloat16")
 declare("bonh", 128, "float16")
 declare("bonf nidf iom ion", 128, "float32")
-declare("dm nd posk kc10 kc11 kc30 kc31 loc ngb xw ptf pts", 256, "float32")
+declare("key kt ksc dm nd posk kc1 kc3 loc ngb xw ptf pts", 256, "float32")
 declare("ioa iob ioc iod ioe iof dwb", 256, "float32", "iox")
 declare("kr ptx parh", 256, "float16")
 declare("zero k0 sg g2 dc dr", 256, "bfloat16")
 declare("lo lo2 bb xi xi2 oo t2 pl", 256, "int32")
 declare("lst pu", 256, "uint16")
-declare("cl posu ku fixu paru wlu", 16, "uint16")
+declare("cl bl posu ku fixu paru wlu", 16, "uint16")
+declare("uu qq", 16, "int32")
+declare("kar t1", 256, "float32")
+declare("land1 land2 land3 land4", 512, "bfloat16")
 declare("expct posf npt win", 16, "float32")
 declare("dump wdump c37 dumpf kk onn ps4 de de2 f1 f2 wd w1 w2", 16, "float32", "tin")
 declare("fail", 16, "bfloat16")
@@ -61,11 +64,11 @@ declare("bt", 4, "float32")
 declare("lim", 2, "float32")
 declare("io16", 80, "float32")
 declare("dw1 dw2 dw3 dw4", 256, "float32")
-declare("send1 send2 send3 send4 land1 land2 land3 land4", 256, "bfloat16")
+declare("send1 send2 send3 send4", 256, "bfloat16")
 PSB = ("psS", "psC", "psU", "psK", "psB0", "psB1", "psG", "psX")
 for _n in PSB:
     SCRATCH[_n] = ("psum", [128, 512], "float32")
-SEMAPHORES = ["qv", "qp", "qs", "qg", "snt"] + ["d%d" % k for k in range(8)] + ["arr%d" % k for k in range(1, NR + 1)]
+SEMAPHORES = ["qv", "qp", "qs", "qg", "snt"] + ["d%d" % k for k in range(16)] + ["arr%d" % k for k in range(1, NR + 1)]
 QSEM = {"V": "qv", "P": "qp", "S": "qs", "G": "qg"}
 CACHE = {}
 
@@ -215,29 +218,27 @@ def build():
     CP(pc(0), p0)
     CP(C("pcol", 1, 4), C("pi0", 1, 4))
     pb, pg, ph = pc(1), pc(2), pc(3)
-    TS(pc(4), ph, 0.0, A.is_equal, -BIG, A.mult)
-    TS(pc(5), ph, 1.0, A.is_equal, -BIG, A.mult)
+    TS(pc(4), ph, 0.0, A.is_equal)
+    TS(pc(5), ph, 1.0, A.is_equal)
     TS(pc(6), pb, -1.0, A.mult)
-    TS(pc(7), pb, 16.0, A.mult)
+    TS(pc(7), pb, -16.0, A.mult)
     TS(ALL("bg"), ALL("iog"), pg, A.is_equal)
     CP(C("z1", 15, 143, 16), ALL("bg"))
     TS(ALL("idn"), ALL("iom"), pc(0), A.is_equal)
     SI(ALL("nidn"), ALL("idn"), scale=-1.0)
-    TT(pc(8), pc(5), pb, A.subtract)
-    TT(pc(9), pc(4), pb, A.subtract)
-    TT(pc(10), pc(5), pc(7), A.subtract)
-    TT(pc(11), pc(4), pc(7), A.subtract)
+    TS(pc(8), pc(0), -16.0, A.add)
+    TS(pc(9), pc(0), 16.0, A.add)
     x = cset("bri", 1)
     TS(ALL("bb"), x, 4095, A.bitwise_and)
     TS(ALL("k0"), x, 4096.0, A.is_lt, float(ZC), A.mult)
     TT(ALL("oo"), ALL("bb"), ALL("k0"), A.max)
     CP(ALL("lst"), ALL("oo"))
     SI(ALL("z4k"), ALL("z1"), scale=4096.0)
+    SI(ALL("kc1"), ALL("iob"), bias=pc(6))
+    SI(ALL("kc3"), ALL("iod"), bias=pc(7))
     for h in range(2):
-        SI(ALL("kc1%d" % h), ALL("iob"), bias=pc(8 + h))
-        SI(ALL("kc3%d" % h), ALL("iod"), bias=pc(10 + h))
-    MS(ALL("seg32"), 1.0)
-    MS(C("seg32", 0, 512, 32), 0.0)
+        for gg in range(2):
+            TS(ALL("to%d%d" % (h, gg)), ALL("iom"), (pc(0), pc(9), pc(8))[gg - h], A.is_equal, (pc(4), pc(5))[h], A.mult)
     MS(ALL("zero"), 0.0)
     MS(C("lim", 0, 1), 4.0)
     MS(C("lim", 1, 2), 8.0)
@@ -249,6 +250,7 @@ def build():
     SI(ALL("wz"), ALL("z1"), scale=ALL("wtf"))
     TS(ALL("kr"), ALL("ioa"), pc(6), A.is_equal, ALL("kaf"), A.mult)
     MM(C("psK", 0, 256), ALL("bonh"), ALL("kr"), group())
+    SI(ALL("kar"), C("psK", 0, 256))
     for t in range(1, NR):
         SI(C("bt", t, t + 1), pb, bias=-4.0 * t)
     SI(pc(12), pb, scale=37.0)
@@ -266,6 +268,7 @@ def build():
         o += 4 * L
     SI(ALL("wdump"), C("io16", 48, 64), bias=pb)
     CP(ALL("cl"), C("io16", 64, 80))
+    TS(ALL("bl"), C("io16", 64, 80), 0.0, A.mult, pb, A.add)
     SI(ALL("bonf"), ALL("bon"))
     SI(ALL("ones"), C("seg", 0, 128), scale=0.0, bias=1.0)
     SI(ALL("posk"), ALL("ioe"), bias=pb)
@@ -285,25 +288,30 @@ def build():
                 CP(out, win)
             else:
                 S(out, win, F.Copy, after=share if c >= EARLY else ())
-        for q in range(8):
-            bank = (("psB0", "psB1") if t > 1 else ("psB0", "psB1", "psC", "psU"))[q % (2 if t > 1 else 4)]
+        units = [(0, q, 2048) for q in range(8)] + [(2048, q, 2048) for q in range(8)]
+        if t > 1:
+            units = [(a, q, 2048) for a in (0, 2048) for q in range(HALF)] + [(0, q, 4096) for q in range(HALF, 8)]
+        for z, (a, q, w) in enumerate(units):
+            bank = ("psB0", "psB1", "psK", "psC")[z % (3 if t > 1 else 4)]
+            gr = group()
+            MM(C(bank, 0, w // 8), ALL("idn"), C("pick", a + q, a + w, 8), gr)
             for j in range(2):
-                gr = group()
-                MM(C(bank, 256 * j, 256 * j + 256), ALL("idn"), C("pick", 2 * q + j, 4096, 16), gr)
-                MM(C(bank, 256 * j, 256 * j + 256), ALL("nidn"), cset("capb", t), gr)
-            for j in range(2):
-                out, src = C("over", 2 * q + j, 4096, 16), C(bank, 256 * j, 256 * j + 256)
-                if t == 1 and q % 2:
-                    TS(out, src, 0.0, A.max)
-                else:
-                    S(out, src, F.Relu)
+                MM(C(bank, j, w // 8, 2), ALL("nidn"), C("capb", t - 1 + a // 4, (a + w) // 4, 4), gr)
+                ops[-1]["after"] = (len(ops) - 2 - j,)
+            if t == 1 and z % 2:
+                TS(C("over", a + q, a + w, 8), C(bank, 0, w // 8), 0.0, A.max)
+            else:
+                S(C("over", a + q, a + w, 8), C(bank, 0, w // 8), F.Relu)
 
-    def argmax(src, kc):
-        for h in range(2):
-            TT(R("key", slice(None), slice(16 * h, 16 * h + 16)), src, ALL(kc + "%d" % h), A.add)
+    def argmax(src, kc, bank):
+        TT(ALL("key"), src, ALL(kc), A.add)
         V("transpose", ALL("kt"), ALL("key"))
-        SCAN(ALL("ksc"), ALL("seg32"), ALL("kt"), A.mult, A.max)
-        CP(ALL("ki"), C("ksc", 31, 512, 32))
+        SCAN(ALL("ksc"), C("seg", 0, 256), ALL("kt"), A.mult, A.max)
+        for h in range(2):
+            gr = group()
+            for gg in range(2):
+                MM(C(bank, 48 + h, 64, 2), ALL("to%d%d" % (h, gg)), C("ksc", 16 * gg + 15, 256, 32), gr)
+        CP(ALL("ki"), C(bank, 48, 64))
 
     def step1(t):
         n1 = 16 * HS
@@ -324,7 +332,7 @@ def build():
         gr = group()
         for b in range(16):
             MM(C("psU", 16, 32), C("z1", 15 - b, 143 - b), C("sg", b, 256, 16), gr)
-        argmax(C("psS", 0, 256), "kc1")
+        argmax(C("psS", 0, 256), "kc1", "psB0")
         TS(ALL("kj"), ALL("ki"), 4095, A.bitwise_and)
         TS(ALL("fail"), C("psU", 16, 32), C("lim", 1, 2), A.add, 0.0, A.is_gt)
         TT(ALL("dumpf"), ALL("dump"), ALL("fail"), A.subtract)
@@ -391,42 +399,46 @@ def build():
 
     def step3(t):
         ln = "land%d" % t
-        la = ALL(ln)
+        la = C(ln, 0, 256)
         add("arr", "arr", (t,), {}, [], [la], 3500)
         gr = group()
         for b in range(16):
             MM(C("psU", 0, 16), C("wz", 15 - b, 143 - b), C(ln, b, 256, 16), gr)
         TT(ALL("x16"), C("psU", 0, 16), ALL("c37"), A.add)
-        u16 = R("uq", 0, slice(0, 16))
+        u16, q16 = ALL("uu"), ALL("qq")
         TS(u16, ALL("x16"), 4095, A.bitwise_and)
         TT(ALL("sq"), u16, u16, A.mult)
-        TS(R("uq", 1, slice(0, 16)), ALL("sq"), 5, A.arith_shift_right)
-        for w in (16, 32, 64, 128):
-            CP(R("uq", slice(None), slice(w, 2 * w)), R("uq", slice(None), slice(0, w)))
-        TT(C("psK", 256, 512), R("uq", 0, slice(0, 256)), C("psK", 0, 256), A.mult)
-        TT(ALL("t2"), C("psK", 256, 512), R("uq", 1, slice(0, 256)), A.add)
+        TT(ALL("t1"), IND(u16, ALL("bl")), ALL("kar"), A.mult)
+        TS(q16, ALL("sq"), 5, A.arith_shift_right)
+        TT(ALL("t2"), IND(q16, ALL("bl")), ALL("t1"), A.add)
         TS(ALL("pl"), ALL("t2"), 1023, A.bitwise_and)
         CP(ALL("pu"), ALL("pl"))
         gr = group()
-        nv = 16 - SM
+        nv = 16 - (SM if t < NR else SML)
         share = []
-        for m in range(nv, 16):
-            S(C("slg", 256 * m, 256 * m + 256), IND(ALL("slack"), C("pu", 16 * m, 16 * m + 16)), F.Copy)
+        DMA("Y", C(ln, 256, 512), la, 2000)
+        for m in range(nv, 16, 2):
+            e = min(m + 2, 16)
+            S(C("slg", 256 * m, 256 * e), IND(ALL("slack"), C("pu", 16 * m, 16 * e)), F.Copy)
             share.append(len(ops) - 1)
         for m in range(nv):
-            TT(C("mins", 256 * m, 256 * m + 256), IND(ALL("slack"), C("pu", 16 * m, 16 * m + 16)), la, A.min)
+            if m % 2 == 0:
+                e = min(m + 2, nv)
+                TT(C("mins", 256 * m, 256 * e), IND(ALL("slack"), C("pu", 16 * m, 16 * e)), C(ln, 0, 256 * (e - m)), A.min)
             MM(C("psC", 0, 256), C("z256", m, m + 128), C("mins", 256 * m, 256 * m + 256), gr)
-        for m in range(nv, 16):
-            h = 256 * (m % 2)
-            bank = "psG" if m % 2 else "psS"
+        for m in range(nv, 16, 2):
+            e = min(m + 2, 16)
+            w = 256 * (e - m)
+            bank = "psG" if (m - nv) % 4 else "psS"
             g2 = group()
-            MM(C(bank, h, h + 256), ALL("idn"), la, g2)
-            MM(C(bank, h, h + 256), ALL("nidn"), C("slg", 256 * m, 256 * m + 256), g2)
-            MM(C("psC", 0, 256), C("z256", m, m + 128), la, gr)
-            S(C("mins", 256 * m, 256 * m + 256), C(bank, h, h + 256), F.Relu)
+            MM(C(bank, 0, w), ALL("idn"), C(ln, 0, w), g2)
+            MM(C(bank, 0, w), ALL("nidn"), C("slg", 256 * m, 256 * e), g2)
+            S(C("mins", 256 * m, 256 * e), C(bank, 0, w), F.Relu)
             share.append(len(ops) - 1)
-            MM(C("psC", 0, 256), C("nz256", m, m + 128), C("mins", 256 * m, 256 * m + 256), gr)
-        argmax(C("psC", 0, 256), "kc3")
+            for c in range(m, e):
+                MM(C("psC", 0, 256), C("z256", c, c + 128), la, gr)
+                MM(C("psC", 0, 256), C("nz256", c, c + 128), C("mins", 256 * c, 256 * c + 256), gr)
+        argmax(C("psC", 0, 256), "kc3", "psU")
         TS(ALL("kj"), ALL("ki"), 255, A.bitwise_and)
         CP(ALL("ku"), ALL("kj"))
         TT(ALL("ptx"), IND(ALL("pl"), ALL("ku")), ALL("dm"), A.mult)
@@ -438,7 +450,7 @@ def build():
         o = 0
         for a in range(16):
             L = 64 * (a // 4 + 1)
-            if a >= 16 - SA:
+            if a >= 16 - (SA if t < NR else SAL):
                 S(C("eq", o, o + L), C("psX", 0, L), F.Abs, scale=1024.0, bias=C("npt", a, a + 1))
             else:
                 TS(C("eq", o, o + L), C("parh", 0, L), C("pts", 16 * a + 15, 16 * a + 16), A.not_equal, 1024.0, A.mult)
@@ -488,6 +500,7 @@ def build():
     return ops
 
 
+WINDOW = 100
 LAT = 90
 
 
@@ -539,6 +552,7 @@ def schedule(ops, deps, order):
     prio = [0.0] * n
     for i in range(n - 1, -1, -1):
         prio[i] = ops[i]["dur"] + LAT + max([prio[k] for k in nxt[i]] + [0.0])
+        prio[i] -= 0.001 * i
     left = [len(p) for p in pre]
     ready, est, free, out = {}, [0.0] * n, {}, []
     fin, start = [0.0] * n, [0.0] * n
@@ -552,7 +566,7 @@ def schedule(ops, deps, order):
                 continue
             f = 0.0 if q == "arr" else free.get(q, 0.0)
             e = min(max(f, est[i]) for i in lst)
-            c = max((i for i in lst if max(f, est[i]) <= e + 250), key=lambda i: prio[i])
+            c = max((i for i in lst if max(f, est[i]) <= e + WINDOW), key=lambda i: prio[i])
             if best is None or max(f, est[c]) < best[0]:
                 best = (max(f, est[c]), q, c)
         s, q, c = best
@@ -568,6 +582,39 @@ def schedule(ops, deps, order):
     return out, start, fin
 
 
+def improve(ops, deps, order, start, fin, rounds=8):
+    n = len(ops)
+    pre = [[(j, LAT if j in deps[i] or ops[i]["m"] == "arr" else 0.0) for j in deps[i] | order[i]] for i in range(n)]
+    suc = [[] for _ in range(n)]
+    for i in range(n):
+        for j, lat in pre[i]:
+            suc[j].append((i, lat))
+    best = (max(fin), list(start))
+
+    def pack(seq, edges):
+        busy, s0, f0 = {}, [0.0] * n, [0.0] * n
+        for i in seq:
+            t = max([f0[j] + lat for j, lat in edges[i]] + [0.0])
+            d, q = ops[i]["dur"], ops[i]["q"]
+            if q in "VPSG" and ops[i]["m"] != "dma_start":
+                lst = busy.setdefault(q, [])
+                k = len(lst)
+                while k and lst[k - 1][1] > t:
+                    k -= 1
+                while k < len(lst) and lst[k][0] < t + d:
+                    t = max(t, lst[k][1])
+                    k += 1
+                lst.insert(k, (t, t + d))
+            s0[i], f0[i] = t, t + d
+        return s0, f0
+    for _ in range(rounds):
+        s1, f1 = pack(sorted(range(n), key=lambda i: (-fin[i], -i)), suc)
+        start, fin = pack(sorted(range(n), key=lambda i: (-f1[i], i)), pre)
+        if max(fin) < best[0]:
+            best = (max(fin), list(start))
+    return sorted(range(n), key=lambda i: (best[1][i], i)), best[0]
+
+
 def rank_program(g, core, T, topo):
     rank = T.rank_of(core)
     if rank is None:
@@ -575,7 +622,7 @@ def rank_program(g, core, T, topo):
     if "plan" not in CACHE:
         ops = build()
         deps, order = depend(ops)
-        seq, start, fin = schedule(ops, deps, order)
+        seq, end = improve(ops, deps, order, *schedule(ops, deps, order)[1:])
         first, last = {}, {}
         for i in seq:
             gr = ops[i]["grp"]
@@ -625,7 +672,7 @@ def rank_program(g, core, T, topo):
             t = op["args"][0]
             dst = T.cores[(rank + 1 + (t - 1) % (n - 1)) % n]
             rid, pid = topo.addr(dst, core)
-            g.remote_dma(out_ap=T["land%d" % t][:], in_ap=T["send%d" % t][:], remote_sem=T.sem["arr%d" % t], local_sem=T.sem.snt,
+            g.remote_dma(out_ap=T["land%d" % t][:, 0:256], in_ap=T["send%d" % t][:], remote_sem=T.sem["arr%d" % t], local_sem=T.sem.snt,
                          pid=pid, routing_id=rid, dma_engine_mask=topo.mask(core, dst))
             total["snt"] = total.get("snt", 0) + len(topo.engines(core, dst))
             comp[i] = ("snt", 10 ** 6)

import numpy as np
from concourse.mybir import dt, AluOpType as A, AxisListType, ActivationFunctionType as F

NR, NQ, ZC = 4, 256, 1792
SM = 4
HALF = 2
EARLY = 5
SA = 5
SML, SAL = 6, 5
HS = 256

SCRATCH = {
    "resw": ("sbuf", [128, 1808], "bfloat16"),
    "capb": ("sbuf", [128, 1024], "bfloat16"),
    "slack": ("sbuf", [128, 1024], "bfloat16"),
    "bri": ("sbuf", [128, 1024], "int32"),
    "words": ("sbuf", [128, 1280], "float32"),
    "pick": ("sbuf", [128, 4352], "bfloat16"), "over": ("sbuf", [128, 4352], "bfloat16"),
    "scn": ("sbuf", [128, 4096], "bfloat16"), "mins": ("sbuf", [128, 4096], "bfloat16"),
    "slg": ("sbuf", [128, 4096], "bfloat16"),
    "eq": ("sbuf", [128, 2560], "bfloat16"), "fs": ("sbuf", [128, 2560], "float16"),
    "seg": ("sbuf", [128, 2048], "bfloat16"), "inc": ("sbuf", [128, 2560], "bfloat16"),
}


PART = {}


def declare(names, cols, dtype, pool=None):
    for j, nm in enumerate(names.split()):
        if pool is None:
            SCRATCH[nm] = ("sbuf", [128, cols], dtype)
        else:
            SCRATCH[pool] = ("sbuf", [128, cols * (j + 1)], dtype)
            PART[nm] = (pool, cols * j, cols * (j + 1))


declare("wti kai ai aj", 1, "int32")
declare("wtf kaf asum", 1, "float32")
declare("to00 to01 to10 to11", 128, "float32")
declare("z1 z4k z256 nz256 wz", 144, "bfloat16")
declare("idn nidn ones bon", 128, "bfloat16")
declare("bonh", 128, "float16")
declare("bonf nidf iom ion", 128, "float32")
declare("key kt ksc dm nd posk kc1 kc3 loc ngb xw ptf pts", 256, "float32")
declare("ioa iob ioc iod ioe iof dwb", 256, "float32", "iox")
declare("kr ptx parh", 256, "float16")
declare("zero k0 sg g2 dc dr", 256, "bfloat16")
declare("lo lo2 bb xi xi2 oo t2 pl", 256, "int32")
declare("lst pu", 256, "uint16")
declare("cl bl posu ku fixu paru wlu", 16, "uint16")
declare("uu qq", 16, "int32")
declare("kar t1", 256, "float32")
declare("land1 land2 land3 land4", 512, "bfloat16")
declare("expct posf npt win", 16, "float32")
declare("dump wdump c37 dumpf kk onn ps4 de de2 f1 f2 wd w1 w2", 16, "float32", "tin")
declare("fail", 16, "bfloat16")
declare("ki kj x16 sq pi r3", 16, "int32")
declare("bg", 8, "bfloat16")
declare("iog", 8, "float32")
declare("pcol", 16, "float32")
declare("pi0", 4, "int32")
declare("bt", 4, "float32")
declare("lim", 2, "float32")
declare("io16", 80, "float32")
declare("dw1 dw2 dw3 dw4", 256, "float32")
declare("send1 send2 send3 send4", 256, "bfloat16")
PSB = ("psS", "psC", "psU", "psK", "psB0", "psB1", "psG", "psX")
for _n in PSB:
    SCRATCH[_n] = ("psum", [128, 512], "float32")
SEMAPHORES = ["qv", "qp", "qs", "qg", "snt"] + ["d%d" % k for k in range(16)] + ["arr%d" % k for k in range(1, NR + 1)]
QSEM = {"V": "qv", "P": "qp", "S": "qs", "G": "qg"}
CACHE = {}


def R(name, *idx):
    return ("ap", name, idx)


def C(name, a, b, st=1):
    return ("ap", name, (slice(a, b, st),))


def ALL(name):
    return C(*PART[name]) if name in PART else ("ap", name, ())


def IND(win, off):
    return ("ind", win, off)


def cols_of(x):
    shp = SCRATCH[x[1]][1][1:]
    n = int(np.prod(shp))
    return n, np.arange(n).reshape(shp)[x[2]].ravel()


def size(x):
    return size(x[2]) * 16 if x[0] == "ind" else cols_of(x)[1].size


def build():
    ops = []

    def add(q, m, args, kw, reads, writes, dur, grp=None):
        ops.append({"q": q, "m": m, "args": args, "kw": kw, "r": reads, "w": writes, "dur": dur, "grp": grp, "tag": m})

    def split(out, ins):
        rd, wr = [], []
        for x in ins:
            if isinstance(x, tuple):
                rd += [x[1], x[2]] if x[0] == "ind" else [x]
        if out[0] == "ind":
            rd.append(out[2])
            wr.append(out[1])
        else:
            wr.append(out)
        return rd, wr

    def V(m, out, *ins, **kw):
        rd, wr = split(out, ins)
        n = size(out)
        if m == "tensor_tensor":
            cyc = n if any(x[1] in PSB for x in ins[:2]) else 2 * n
        elif m == "tensor_reduce":
            cyc = size(ins[0])
        else:
            wide = [x for x in (out,) + ins if isinstance(x, tuple) and x[0] == "ap" and size(x) > 1 and SCRATCH[x[1]][2] in ("float32", "int32")]
            cyc = n if wide else n / 2
        if out[0] == "ind":
            cyc = 3.0 * n
        if any(isinstance(x, tuple) and x[0] == "ind" for x in ins):
            cyc = 1.56 * n
        add("V", m, (out,) + ins, kw, rd, wr, 60 + 1.04 * max(cyc, 64))

    def TT(out, a, b, op):
        V("tensor_tensor", out, a, b, op)

    def TS(out, a, s1, op0, s2=None, op1=None):
        if op1 is None:
            V("tensor_scalar", out, a, s1, None, op0)
        else:
            V("tensor_scalar", out, a, s1, s2, op0, op1)

    def CP(out, a):
        V("tensor_copy", out, a)

    def MS(out, val):
        V("memset", out, val)

    def SCAN(out, d0, d1, o0, o1):
        V("tensor_tensor_scan", out, d0, d1, 0.0, o0, o1)

    def S(out, a, func, after=(), **kw):
        rd, wr = split(out, [a] + list(kw.values()))
        c = 1.56 * size(a) if a[0] == "ind" else size(a)
        add("S", "activation", (out, a, func), kw, rd, wr, 65 + 1.04 * max(c, 64))
        if after:
            ops[-1]["after"] = after

    def SI(out, a, **kw):
        S(out, a, F.Identity, **kw)

    ng = [0]

    def group():
        ng[0] += 1
        return ng[0]

    def MM(out, l, r, grp):
        f4 = 4 if SCRATCH[r[1]][2] == "float32" else 1
        add("P", "matmul", (out, l, r), {}, [l, r], [out], 10 + f4 * max(64, size(r)) * 0.5, grp)

    def IOTA(out, pattern, base, cm):
        kw = {} if SCRATCH[out[1]][2] == "int32" else {"allow_small_or_imprecise_dtypes": True}
        add("G", "iota", (out, pattern, base, cm), kw, [], [out], 130 + 2 * size(out))

    nd = [0]

    def DMA(q, out, in_, dur):
        add(q, "dma_start", (out, in_), {}, [in_] if in_[1] in SCRATCH else [], [out] if out[1] in SCRATCH else [], dur)
        ops[-1]["sem"] = "d%d" % nd[0]
        nd[0] += 1

    def cset(n, s):
        return C(n, s - 1, 1024, 4)

    DMA("Y", ALL("bri"), ALL("br"), 4000)
    DMA("Y", C("resw", 0, ZC), ALL("res"), 4500)
    DMA("S", ALL("capb"), ALL("cap"), 4000)
    DMA("S", ALL("kai"), ALL("ka"), 2000)
    DMA("S", ALL("wti"), ALL("wt"), 2000)
    p0 = C("pi0", 0, 1)

    def pc(j):
        return C("pcol", j, j + 1)
    IOTA(p0, [[0, 1]], 0, 1)
    IOTA(ALL("iog"), [[1, 8]], 0, 0)
    IOTA(ALL("iom"), [[1, 128]], 0, 0)
    IOTA(ALL("ion"), [[1, 8], [0, 16]], 0, 0)
    IOTA(ALL("iob"), [[-15, 256]], 4095, 0)
    IOTA(C("io16", 0, 16), [[16, 16]], 4096, 0)
    IOTA(C("io16", 16, 32), [[592, 16]], 0, 0)
    IOTA(C("io16", 32, 48), [[0, 4], [16, 4]], -63, 0)
    IOTA(C("io16", 48, 64), [[16, 16]], 1024, 0)
    IOTA(C("io16", 64, 80), [[1, 16]], 0, 0)
    IOTA(ALL("ioa"), [[1, 16], [0, 16]], -15, 0)
    IOTA(ALL("ioc"), [[0, 16], [1, 16]], 0, 0)
    IOTA(ALL("iod"), [[1, 16], [0, 16]], 240, 0)
    IOTA(ALL("ioe"), [[16, 256]], 0, 0)
    MS(C("resw", ZC, ZC + 16), 0.0)
    MS(ALL("seg"), 1.0)
    MS(C("seg", 0, 2048, 16), 0.0)
    MS(ALL("z1"), 0.0)
    TS(C("pi0", 1, 2), p0, 15, A.bitwise_and)
    TS(C("pi0", 2, 3), p0, 4, A.arith_shift_right)
    TS(C("pi0", 3, 4), C("pi0", 2, 3), 1, A.bitwise_and)
    CP(pc(0), p0)
    CP(C("pcol", 1, 4), C("pi0", 1, 4))
    pb, pg, ph = pc(1), pc(2), pc(3)
    TS(pc(4), ph, 0.0, A.is_equal)
    TS(pc(5), ph, 1.0, A.is_equal)
    TS(pc(6), pb, -1.0, A.mult)
    TS(pc(7), pb, -16.0, A.mult)
    TS(ALL("bg"), ALL("iog"), pg, A.is_equal)
    CP(C("z1", 15, 143, 16), ALL("bg"))
    TS(ALL("idn"), ALL("iom"), pc(0), A.is_equal)
    SI(ALL("nidn"), ALL("idn"), scale=-1.0)
    TS(pc(8), pc(0), -16.0, A.add)
    TS(pc(9), pc(0), 16.0, A.add)
    x = cset("bri", 1)
    TS(ALL("bb"), x, 4095, A.bitwise_and)
    TS(ALL("k0"), x, 4096.0, A.is_lt, float(ZC), A.mult)
    TT(ALL("oo"), ALL("bb"), ALL("k0"), A.max)
    CP(ALL("lst"), ALL("oo"))
    SI(ALL("z4k"), ALL("z1"), scale=4096.0)
    SI(ALL("kc1"), ALL("iob"), bias=pc(6))
    SI(ALL("kc3"), ALL("iod"), bias=pc(7))
    for h in range(2):
        for gg in range(2):
            TS(ALL("to%d%d" % (h, gg)), ALL("iom"), (pc(0), pc(9), pc(8))[gg - h], A.is_equal, (pc(4), pc(5))[h], A.mult)
    MS(ALL("zero"), 0.0)
    MS(C("lim", 0, 1), 4.0)
    MS(C("lim", 1, 2), 8.0)
    SI(ALL("dump"), C("io16", 0, 16), bias=pb)
    TS(ALL("bon"), ALL("ion"), pg, A.is_equal)
    CP(ALL("bonh"), ALL("bon"))
    CP(ALL("kaf"), ALL("kai"))
    CP(ALL("wtf"), ALL("wti"))
    SI(ALL("wz"), ALL("z1"), scale=ALL("wtf"))
    TS(ALL("kr"), ALL("ioa"), pc(6), A.is_equal, ALL("kaf"), A.mult)
    MM(C("psK", 0, 256), ALL("bonh"), ALL("kr"), group())
    SI(ALL("kar"), C("psK", 0, 256))
    for t in range(1, NR):
        SI(C("bt", t, t + 1), pb, bias=-4.0 * t)
    SI(pc(12), pb, scale=37.0)
    SI(ALL("c37"), C("io16", 16, 32), bias=pc(12))
    SI(ALL("z256"), ALL("z1"), scale=256.0)
    SI(ALL("nz256"), ALL("z1"), scale=-256.0)
    TS(ALL("dm"), ALL("ioc"), pb, A.is_equal)
    SI(ALL("expct"), C("io16", 32, 48), bias=pb)
    SI(C("inc", 0, 2048), ALL("seg"), scale=0.0, bias=-1.0)
    SI(C("inc", 2048, 2560), C("seg", 0, 512), scale=0.0, bias=-1.0)
    o = 0
    for qd in range(4):
        L = 64 * (qd + 1)
        SI(C("inc", o, o + 4 * L, L), C("seg", 0, 4), scale=0.0, bias=1024.0)
        o += 4 * L
    SI(ALL("wdump"), C("io16", 48, 64), bias=pb)
    CP(ALL("cl"), C("io16", 64, 80))
    TS(ALL("bl"), C("io16", 64, 80), 0.0, A.mult, pb, A.add)
    SI(ALL("bonf"), ALL("bon"))
    SI(ALL("ones"), C("seg", 0, 128), scale=0.0, bias=1.0)
    SI(ALL("posk"), ALL("ioe"), bias=pb)
    SI(ALL("nidf"), ALL("idn"), scale=-1.0)
    SI(ALL("nd"), ALL("dm"), scale=-1.0, bias=1.0)
    CP(C("words", 0, 1024), ALL("bri"))
    IOTA(ALL("iof"), [[1, 256]], -2 ** 20, 0)
    SI(ALL("xw"), ALL("dm"), scale=float(2 ** 20))
    TT(ALL("dwb"), ALL("xw"), ALL("iof"), A.add)
    for t in range(1, NR + 1):
        S(ALL("dw%d" % t), ALL("dwb"), F.Relu, bias=1024.0 + 256 * (t - 1) + 4096 * (t + 2))

    def background(t, share=()):
        for c in range(8):
            out, win = C("pick", 512 * c, 512 * c + 512), IND(C("resw", 0, 1808), C("lst", 32 * c, 32 * c + 32))
            if t == 1 and c % 2:
                CP(out, win)
            else:
                S(out, win, F.Copy, after=share if c >= EARLY else ())
        units = [(0, q, 2048) for q in range(8)] + [(2048, q, 2048) for q in range(8)]
        if t > 1:
            units = [(a, q, 2048) for a in (0, 2048) for q in range(HALF)] + [(0, q, 4096) for q in range(HALF, 8)]
        for z, (a, q, w) in enumerate(units):
            bank = ("psB0", "psB1", "psK", "psC")[z % (3 if t > 1 else 4)]
            gr = group()
            MM(C(bank, 0, w // 8), ALL("idn"), C("pick", a + q, a + w, 8), gr)
            for j in range(2):
                MM(C(bank, j, w // 8, 2), ALL("nidn"), C("capb", t - 1 + a // 4, (a + w) // 4, 4), gr)
                ops[-1]["after"] = (len(ops) - 2 - j,)
            if t == 1 and z % 2:
                TS(C("over", a + q, a + w, 8), C(bank, 0, w // 8), 0.0, A.max)
            else:
                S(C("over", a + q, a + w, 8), C(bank, 0, w // 8), F.Relu)

    def argmax(src, kc, bank):
        TT(ALL("key"), src, ALL(kc), A.add)
        V("transpose", ALL("kt"), ALL("key"))
        SCAN(ALL("ksc"), C("seg", 0, 256), ALL("kt"), A.mult, A.max)
        for h in range(2):
            gr = group()
            for gg in range(2):
                MM(C(bank, 48 + h, 64, 2), ALL("to%d%d" % (h, gg)), C("ksc", 16 * gg + 15, 256, 32), gr)
        CP(ALL("ki"), C(bank, 48, 64))

    def step1(t):
        n1 = 16 * HS
        for a in range(0, n1, 2048):
            w = min(2048, n1 - a)
            SCAN(C("scn", a, a + w), C("seg", 0, w), C("pick", a, a + w), A.mult, A.max)
        gr = group()
        for k in range(16):
            MM(C("psS", 0, 256), C("z4k", 15 - k, 143 - k), C("over", k, 4096, 16), gr)
        if HS < NQ:
            gr = group()
            for k in range(16):
                MM(C("psG", HS, NQ), ALL("idn"), C("over", n1 + k, 4096, 16), gr)
        gr = group()
        MM(C("psG", 0, HS), ALL("idn"), C("scn", 15, n1, 16), gr)
        MM(C("psG", 0, HS), ALL("nidn"), C("capb", t - 1, 4 * HS, 4), gr)
        S(ALL("sg"), C("psG", 0, 256), F.Sign, bias=-0.5)
        gr = group()
        for b in range(16):
            MM(C("psU", 16, 32), C("z1", 15 - b, 143 - b), C("sg", b, 256, 16), gr)
        argmax(C("psS", 0, 256), "kc1", "psB0")
        TS(ALL("kj"), ALL("ki"), 4095, A.bitwise_and)
        TS(ALL("fail"), C("psU", 16, 32), C("lim", 1, 2), A.add, 0.0, A.is_gt)
        TT(ALL("dumpf"), ALL("dump"), ALL("fail"), A.subtract)
        TT(ALL("kk"), ALL("kj"), ALL("fail"), A.mult)
        TT(ALL("posf"), ALL("dumpf"), ALL("kk"), A.subtract)
        CP(ALL("posu"), ALL("posf"))
        V("tensor_copy", IND(C("pick", 0, 4352), ALL("posu")), ALL("zero"))
        for a in (0, 2048):
            SCAN(C("scn", a, a + 2048), ALL("seg"), C("pick", a, a + 2048), A.mult, A.max)
        m = C("scn", 15, 4096, 16)
        MM(C("psS", 256, 512), ALL("idn"), cset("capb", t), group())
        TT(ALL("g2"), m, C("psS", 256, 512), A.is_gt)
        MM(C("psX", 0, 256), ALL("bon"), ALL("g2"), group())
        TS(C("psX", 256, 512), C("psX", 0, 256), C("lim", 0, 1), A.is_le)
        sn = ALL("send%d" % t)
        TT(sn, m, C("psX", 256, 512), A.mult)
        add("G", "remote", (t,), {}, [sn], [], 1500)
        S(cset("resw", t), sn, F.Copy)
        gr = group()
        MM(C("psG", 256, 512), ALL("idn"), cset("capb", t), gr)
        MM(C("psG", 256, 512), ALL("nidn"), sn, gr)
        S(cset("slack", t), C("psG", 256, 512), F.Relu)
        if t == NR:
            DMA("Y", ALL("yr"), C("resw", 0, 1024), 3500)
        else:
            MM(C("psU", 32, 48), ALL("ones"), ALL("fail"), group())
            V("tensor_reduce", ALL("asum"), C("psU", 32, 48), AxisListType.X, A.add)
            CP(ALL("ai"), ALL("asum"))
            TS(ALL("aj"), ALL("ai"), 1, A.bitwise_and)
            TS(C("lim", 0, 1), ALL("aj"), 4.0, A.add)
            TS(C("lim", 1, 2), ALL("aj"), -2.0, A.mult, 8.0, A.add)

    def merge(t):
        TT(ALL("w1"), ALL("win"), ALL("wd"), A.mult)
        TT(ALL("w2"), ALL("w1"), ALL("wdump"), A.add)
        CP(ALL("wlu"), ALL("w2"))
        TT(ALL("xw"), IND(C("words", 0, 1024), ALL("paru")), ALL("nd"), A.mult)
        TT(IND(C("words", 0, 1280), ALL("wlu")), ALL("xw"), ALL("dw%d" % t), A.add)

    def suspend(t):
        TT(ALL("ptf"), IND(ALL("posf"), ALL("cl")), ALL("dm"), A.mult)
        gr = group()
        MM(C("psX", 0, 256), ALL("bonf"), ALL("ptf"), gr)
        MM(C("psX", 0, 256), ALL("nidf"), ALL("posk"), gr)
        CP(ALL("xi"), cset("words", t))
        TS(ALL("lo"), ALL("xi"), 65535, A.bitwise_and)
        S(ALL("ngb"), C("psX", 0, 256), F.Square, scale=2048.0)
        S(C("psC", 0, 256), ALL("ngb"), F.Identity, bias=-65536.0 * (t + 4))
        TT(C("psC", 256, 512), ALL("lo"), C("psC", 0, 256), A.add)
        TT(cset("words", t), cset("words", t), C("psC", 256, 512), A.min)

    def makelist(s):
        x = cset("bri", 2)
        if s > 2:
            x = ALL("xi2")
            CP(x, cset("words", s))
        S(ALL("loc"), cset("words", s), F.Relu, scale=-2048.0, bias=-2048.0 * 65536.0 * (s - 1))
        TS(ALL("lo2"), x, 65535, A.bitwise_and)
        TS(ALL("bb"), x, 4095, A.bitwise_and)
        TS(C("psS", 0, 256), ALL("lo2"), 4096.0 * s, A.is_lt, float(ZC), A.mult)
        TT(C("psS", 256, 512), C("psS", 0, 256), ALL("loc"), A.max)
        TT(ALL("oo"), C("psS", 256, 512), ALL("bb"), A.max)
        TS(ALL("lst"), ALL("oo"), float(ZC), A.min)

    def step3(t):
        ln = "land%d" % t
        la = C(ln, 0, 256)
        add("arr", "arr", (t,), {}, [], [la], 3500)
        gr = group()
        for b in range(16):
            MM(C("psU", 0, 16), C("wz", 15 - b, 143 - b), C(ln, b, 256, 16), gr)
        TT(ALL("x16"), C("psU", 0, 16), ALL("c37"), A.add)
        u16, q16 = ALL("uu"), ALL("qq")
        TS(u16, ALL("x16"), 4095, A.bitwise_and)
        TT(ALL("sq"), u16, u16, A.mult)
        TT(ALL("t1"), IND(u16, ALL("bl")), ALL("kar"), A.mult)
        TS(q16, ALL("sq"), 5, A.arith_shift_right)
        TT(ALL("t2"), IND(q16, ALL("bl")), ALL("t1"), A.add)
        TS(ALL("pl"), ALL("t2"), 1023, A.bitwise_and)
        CP(ALL("pu"), ALL("pl"))
        gr = group()
        nv = 16 - (SM if t < NR else SML)
        share = []
        DMA("Y", C(ln, 256, 512), la, 2000)
        for m in range(nv, 16, 2):
            e = min(m + 2, 16)
            S(C("slg", 256 * m, 256 * e), IND(ALL("slack"), C("pu", 16 * m, 16 * e)), F.Copy)
            share.append(len(ops) - 1)
        for m in range(nv):
            if m % 2 == 0:
                e = min(m + 2, nv)
                TT(C("mins", 256 * m, 256 * e), IND(ALL("slack"), C("pu", 16 * m, 16 * e)), C(ln, 0, 256 * (e - m)), A.min)
            MM(C("psC", 0, 256), C("z256", m, m + 128), C("mins", 256 * m, 256 * m + 256), gr)
        for m in range(nv, 16, 2):
            e = min(m + 2, 16)
            w = 256 * (e - m)
            bank = "psG" if (m - nv) % 4 else "psS"
            g2 = group()
            MM(C(bank, 0, w), ALL("idn"), C(ln, 0, w), g2)
            MM(C(bank, 0, w), ALL("nidn"), C("slg", 256 * m, 256 * e), g2)
            S(C("mins", 256 * m, 256 * e), C(bank, 0, w), F.Relu)
            share.append(len(ops) - 1)
            for c in range(m, e):
                MM(C("psC", 0, 256), C("z256", c, c + 128), la, gr)
                MM(C("psC", 0, 256), C("nz256", c, c + 128), C("mins", 256 * c, 256 * c + 256), gr)
        argmax(C("psC", 0, 256), "kc3", "psU")
        TS(ALL("kj"), ALL("ki"), 255, A.bitwise_and)
        CP(ALL("ku"), ALL("kj"))
        TT(ALL("ptx"), IND(ALL("pl"), ALL("ku")), ALL("dm"), A.mult)
        MM(C("psX", 0, 256), ALL("bonh"), ALL("ptx"), group())
        SCAN(ALL("pts"), C("seg", 0, 256), ALL("ptx"), A.mult, A.add)
        pt = C("pts", 15, 256, 16)
        CP(ALL("parh"), C("psX", 0, 256))
        SI(ALL("npt"), pt, scale=-1024.0)
        o = 0
        for a in range(16):
            L = 64 * (a // 4 + 1)
            if a >= 16 - (SA if t < NR else SAL):
                S(C("eq", o, o + L), C("psX", 0, L), F.Abs, scale=1024.0, bias=C("npt", a, a + 1))
            else:
                TS(C("eq", o, o + L), C("parh", 0, L), C("pts", 16 * a + 15, 16 * a + 16), A.not_equal, 1024.0, A.mult)
            o += L
        SCAN(ALL("fs"), ALL("inc"), ALL("eq"), A.add, A.min)
        CP(ALL("pi"), pt)
        CP(ALL("paru"), pt)
        if t < NR:
            TT(ALL("dc"), IND(ALL("capb"), ALL("paru")), la, A.subtract)
            S(ALL("dr"), ALL("dc"), F.Relu, scale=-1.0)
            TS(ALL("r3"), ALL("pi"), 3, A.bitwise_and)
            TS(ALL("onn"), ALL("r3"), float(t), A.is_equal)
            SI(ALL("ps4"), pt, scale=4.0, bias=C("bt", t, t + 1))
            TT(ALL("de"), ALL("ps4"), ALL("dump"), A.subtract)
            TT(ALL("de2"), ALL("de"), ALL("onn"), A.mult)
        TT(ALL("wd"), ALL("pi"), ALL("wdump"), A.subtract)
        o = 0
        for qd in range(4):
            L = 64 * (qd + 1)
            TT(C("win", 4 * qd, 4 * qd + 4), C("fs", o + L - 1, o + 4 * L, L), C("expct", 4 * qd, 4 * qd + 4), A.is_equal)
            o += 4 * L
        if t < NR:
            S(C("resw", 1024 + 256 * (t - 1), 1280 + 256 * (t - 1)), la, F.Copy)
            background(t + 1, share)
            TT(ALL("f1"), ALL("win"), ALL("de2"), A.mult)
            TT(ALL("f2"), ALL("f1"), ALL("dump"), A.add)
            CP(ALL("fixu"), ALL("f2"))
            V("tensor_copy", IND(C("over", 0, 4352), ALL("fixu")), ALL("dr"))
            V("tensor_copy", IND(C("pick", 0, 4352), ALL("fixu")), la)

    background(1)
    for c in range(2):
        gr = group()
        MM(C("psX", 0, 512), ALL("idn"), C("capb", 512 * c, 512 * c + 512), gr)
        MM(C("psX", 0, 512), ALL("nidn"), C("resw", 512 * c, 512 * c + 512), gr)
        S(C("slack", 512 * c, 512 * c + 512), C("psX", 0, 512), F.Relu)
    for t in range(1, NR + 1):
        step1(t)
        if t > 1:
            merge(t - 1)
        suspend(t)
        if t < NR:
            makelist(t + 1)
        step3(t)
    merge(NR)
    DMA("Y", ALL("yb"), C("words", 0, 1024), 4500)
    return ops


WINDOW = 100
LAT = 90


def depend(ops):
    hist, deps, order, sends = {}, [], [], {}
    for i, op in enumerate(ops):
        dp, od, acc = set(), set(op.get("after", ())), []
        for w, lst in ((0, op["r"]), (1, op["w"])):
            for x in lst:
                n, cs = cols_of(x)
                m = np.zeros(n, bool)
                m[cs] = True
                acc.append((w, x[1], m))
        for w, nm, m in acc:
            ps = nm in PSB
            for (j, w2, m2) in hist.get(nm, ()):
                o2 = ops[j]
                if ps and op["q"] == "P" and o2["q"] == "P":
                    if o2["grp"] != op["grp"]:
                        od.add(j)
                elif ps and o2["q"] != op["q"]:
                    dp.add(j)
                elif (w or w2) and bool(np.any(m & m2)):
                    dp.add(j)
        for w, nm, m in acc:
            h = hist.setdefault(nm, [])
            if nm in PSB:
                h[:] = h[-140:]
            elif w:
                h[:] = [e for e in h if bool(np.any(e[2] & ~m))]
            h.append((i, w, m))
        if op["m"] == "remote":
            sends[op["args"][0]] = i
        if op["m"] == "arr":
            od.add(sends[op["args"][0]])
        dp.discard(i)
        deps.append(dp)
        order.append(od - dp)
    return deps, order


def schedule(ops, deps, order):
    n = len(ops)
    pre = [deps[i] | order[i] for i in range(n)]
    nxt = [[] for _ in range(n)]
    for i in range(n):
        for j in pre[i]:
            nxt[j].append(i)
    prio = [0.0] * n
    for i in range(n - 1, -1, -1):
        prio[i] = ops[i]["dur"] + LAT + max([prio[k] for k in nxt[i]] + [0.0])
        prio[i] -= 0.001 * i
    left = [len(p) for p in pre]
    ready, est, free, out = {}, [0.0] * n, {}, []
    fin, start = [0.0] * n, [0.0] * n
    for i in range(n):
        if not left[i]:
            ready.setdefault(ops[i]["q"], []).append(i)
    while len(out) < n:
        best = None
        for q, lst in ready.items():
            if not lst:
                continue
            f = 0.0 if q == "arr" else free.get(q, 0.0)
            e = min(max(f, est[i]) for i in lst)
            c = max((i for i in lst if max(f, est[i]) <= e + WINDOW), key=lambda i: prio[i])
            if best is None or max(f, est[c]) < best[0]:
                best = (max(f, est[c]), q, c)
        s, q, c = best
        ready[q].remove(c)
        start[c], fin[c] = s, s + ops[c]["dur"]
        free[q] = s + 100 if ops[c]["m"] == "dma_start" else fin[c]
        out.append(c)
        for k in nxt[c]:
            left[k] -= 1
            est[k] = max(est[k], fin[c] + (LAT if c in deps[k] or ops[k]["m"] == "arr" else 0))
            if not left[k]:
                ready.setdefault(ops[k]["q"], []).append(k)
    return out, start, fin


def improve(ops, deps, order, start, fin, rounds=8):
    n = len(ops)
    pre = [[(j, LAT if j in deps[i] or ops[i]["m"] == "arr" else 0.0) for j in deps[i] | order[i]] for i in range(n)]
    suc = [[] for _ in range(n)]
    for i in range(n):
        for j, lat in pre[i]:
            suc[j].append((i, lat))
    best = (max(fin), list(start))

    def pack(seq, edges):
        busy, s0, f0 = {}, [0.0] * n, [0.0] * n
        for i in seq:
            t = max([f0[j] + lat for j, lat in edges[i]] + [0.0])
            d, q = ops[i]["dur"], ops[i]["q"]
            if q in "VPSG" and ops[i]["m"] != "dma_start":
                lst = busy.setdefault(q, [])
                k = len(lst)
                while k and lst[k - 1][1] > t:
                    k -= 1
                while k < len(lst) and lst[k][0] < t + d:
                    t = max(t, lst[k][1])
                    k += 1
                lst.insert(k, (t, t + d))
            s0[i], f0[i] = t, t + d
        return s0, f0
    for _ in range(rounds):
        s1, f1 = pack(sorted(range(n), key=lambda i: (-fin[i], -i)), suc)
        start, fin = pack(sorted(range(n), key=lambda i: (-f1[i], i)), pre)
        if max(fin) < best[0]:
            best = (max(fin), list(start))
    return sorted(range(n), key=lambda i: (best[1][i], i)), best[0]


def rank_program(g, core, T, topo):
    rank = T.rank_of(core)
    if rank is None:
        return
    if "plan" not in CACHE:
        ops = build()
        deps, order = depend(ops)
        seq, end = improve(ops, deps, order, *schedule(ops, deps, order)[1:])
        first, last = {}, {}
        for i in seq:
            gr = ops[i]["grp"]
            if gr is not None:
                first.setdefault(gr, i)
                last[gr] = i
        CACHE["plan"] = (ops, deps, seq, first, last)
    ops, deps, seq, first, last = CACHE["plan"]
    queues = {"V": g.vector, "P": g.tensor, "S": g.scalar, "G": g, "Y": g.sync}
    call = {"tensor_tensor": g.vector.tensor_tensor, "tensor_scalar": g.vector.tensor_scalar, "tensor_copy": g.vector.tensor_copy,
            "memset": g.vector.memset, "tensor_tensor_scan": g.vector.tensor_tensor_scan, "transpose": g.vector.transpose,
            "tensor_reduce": g.vector.tensor_reduce, "activation": g.scalar.activation, "iota": g.iota}
    n = len(T.cores)

    def res(x):
        if not isinstance(x, tuple):
            return x
        if x[0] == "ind":
            return res(x[1]).indirect(res(x[2]))
        return T[x[1]][(slice(None),) + x[2]]

    count, known, comp, clk, total = {}, {}, {}, {}, {}
    for i in seq:
        op = ops[i]
        q, m = op["q"], op["m"]
        if q == "arr":
            t = op["args"][0]
            k = len(topo.engines(T.cores[(rank - 1 - (t - 1) % (n - 1)) % n], core))
            comp[i], clk[i], total["arr%d" % t] = ("arr%d" % t, k), {}, k
            continue
        kn = known.setdefault(q, {})
        need = {}
        for d in deps[i]:
            s, v = comp[d]
            if kn.get(s, 0) < v and need.get(s, (0, 0))[0] < v:
                need[s] = (v, d)
        for s in sorted(need):
            v, d = need[s]
            if not any(s2 != s and clk[d2].get(s, 0) >= v for s2, (v2, d2) in need.items()):
                queues[q].wait_ge(T.sem[s], v)
        for s, (v, d) in need.items():
            for s2, v2 in list(clk[d].items()) + [(s, v)]:
                if kn.get(s2, 0) < v2:
                    kn[s2] = v2
        clk[i] = dict(kn)
        if m == "remote":
            t = op["args"][0]
            dst = T.cores[(rank + 1 + (t - 1) % (n - 1)) % n]
            rid, pid = topo.addr(dst, core)
            g.remote_dma(out_ap=T["land%d" % t][:, 0:256], in_ap=T["send%d" % t][:], remote_sem=T.sem["arr%d" % t], local_sem=T.sem.snt,
                         pid=pid, routing_id=rid, dma_engine_mask=topo.mask(core, dst))
            total["snt"] = total.get("snt", 0) + len(topo.engines(core, dst))
            comp[i] = ("snt", 10 ** 6)
            continue
        args = [res(x) for x in op["args"]]
        if m == "dma_start":
            s = op["sem"]
            queues[q].dma_start(args[0], args[1]).then_inc(T.sem[s], 16)
            comp[i], total[s] = (s, 16), 16
            continue
        if m == "matmul":
            gr = op["grp"]
            c = g.tensor.matmul(args[0], args[1], args[2], first[gr] == i, last[gr] == i)
        else:
            c = call[m](*args, **{k: res(v) for k, v in op["kw"].items()})
        s = QSEM[q]
        count[q] = count.get(q, 0) + 1
        c.then_inc(T.sem[s], 1)
        comp[i], total[s] = (s, count[q]), count[q]
    for s in sorted(total):
        g.sync.wait_ge(T.sem[s], total[s])
